import numpy as np, ml_dtypes
CORES = [13,21,141,149]
N = 4
BF = ml_dtypes.bfloat16
def gentries(a):
    return np.ascontiguousarray(a.reshape(8, 16, -1).transpose(0, 2, 1)).reshape(8, -1)
def gtable(e):
    e = np.asarray(e); return np.ascontiguousarray(e.reshape(8, -1, 16).transpose(0, 2, 1)).reshape(128, -1).astype(np.int32)
R, A, LV, Q = 512, 2, 2, 128
def level(kids, h):
    return kids[h // LV].reshape(8, LV, R, A)[:, h % LV]
def sizes(kids, runs):
    s = [runs[0].astype(np.int64)]
    for h in range(N * LV):
        s.append(np.sum(s[-1][np.arange(8)[:, None, None], level(kids, h)], axis=-1))
    return s
def parts(kids, s, h, n):
    g = np.arange(8)[:, None]; c = level(kids, h)[g, n]
    e = np.add.accumulate(s[h][g[:, :, None], c], axis=-1)
    return c, np.concatenate([np.zeros_like(e[..., :1]), e[..., :-1]], axis=-1)
def put(d, tops, offs):
    d["top"] = np.stack([gtable(v) for v in tops]); d["off"] = np.stack([gtable(v) for v in offs]); return d
def ask(d, tops, u):
    z = sizes(d["kids"], d["runs"])[-1][np.arange(8)[None, :, None], tops]
    return put(d, tops, np.minimum((u * z).astype(np.int64), z - 1))
def setup_inputs(rng):
    d = {"kids": rng.integers(0, R, (N, 8, LV * A * R)).astype(np.int32), "letter": rng.integers(0, 1 << 24, (N, 8, R)).astype(np.int32), "runs": rng.integers(1, 16, (N, 8, R)).astype(np.int32)}
    return ask(d, rng.integers(0, R, (N, 8, Q)), rng.random((N, 8, Q)))
def setup_inputs_edges(rng):
    d = setup_inputs(rng); k = d["kids"]; d["kids"] = np.where(rng.random(k.shape) < 0.25, rng.choice(np.array([0, R - 1]), k.shape), k).astype(np.int32)
    s = sizes(d["kids"], d["runs"]); tops = rng.integers(0, R, (N, 8, Q)); tops[:, :, 0] = 0; tops[:, :, 1] = R - 1; offs = np.zeros((N, 8, Q), np.int64)
    for r in range(N):
        n = tops[r]; low = rng.integers(0, N * LV + 1, (8, Q)); last = rng.integers(0, 2, (8, Q))
        for h in range(N * LV - 1, -1, -1):
            b = np.where(h < low, last * (A - 1), rng.integers(0, A, (8, Q)))[..., None]
            c, w = parts(d["kids"], s, h, n)
            offs[r] += np.take_along_axis(w, b, -1)[..., 0]; n = np.take_along_axis(c, b, -1)[..., 0]
        offs[r] += last * (s[0][np.arange(8)[:, None], n] - 1)
    return put(d, tops, offs)
def setup_inputs_runs(rng):
    d = setup_inputs(rng); d["runs"] = rng.choice(np.array([1, 15]), (N, 8, R)).astype(np.int32); a, b = rng.permutation(8)[:2]
    d["runs"][0, a] = 15; d["runs"][0, b] = 1
    u = rng.random((N, 8, Q)); m = rng.integers(0, 4, u.shape); u = np.where(m == 0, 0.0, np.where(m == 1, 1.0, u))
    return ask(d, rng.integers(0, R, (N, 8, Q)), u)
def setup_inputs_one(rng):
    d = setup_inputs(rng); k = d["kids"].reshape(N, 8, LV * R, A); t = rng.random((N, 8, LV * R, 1)) < 0.5
    d["kids"] = np.where(t, k[..., :1], k).reshape(N, 8, LV * A * R).astype(np.int32)
    tops = np.repeat(rng.integers(0, R, (N, 8, 1)), Q, axis=2); z = sizes(d["kids"], d["runs"])[-1][np.arange(8)[None, :, None], tops]
    start = (rng.random((N, 8, 1)) * z[:, :, :1]).astype(np.int64)
    offs = (start + np.arange(Q)[None, None, :]) % z; q = rng.integers(0, N)
    offs[q] = np.minimum((rng.random((8, 1)) * z[q]).astype(np.int64), z[q] - 1)
    return put(d, tops, offs)
def setup_inputs_spread(rng):
    d = setup_inputs(rng)
    d["kids"] = np.minimum((R * rng.random((N, 8, LV * A * R)) ** 4).astype(np.int32), R - 1)
    d["letter"] = np.minimum(np.exp2(24 * rng.random((N, 8, R))).astype(np.int32), (1 << 24) - 1)
    d["runs"] = np.minimum(1 + (15 * rng.random((N, 8, R)) ** 3).astype(np.int32), 15).astype(np.int32)
    return ask(d, np.minimum((R * rng.random((N, 8, Q)) ** 3).astype(np.int64), R - 1), rng.random((N, 8, Q)) ** 2)
def check_inputs(d):
    bad = []
    for k, lo, hi in (("kids", 0, R - 1), ("letter", 0, (1 << 24) - 1), ("runs", 1, 15), ("top", 0, R - 1)):
        if d[k].min() < lo or d[k].max() > hi: bad.append(k)
    if bad: return bad
    z = sizes(d["kids"], d["runs"])[-1]
    for r in range(N):
        o = gentries(d["off"][r]); n = gentries(d["top"][r])
        if (o < 0).any() or (o >= z[np.arange(8)[:, None], n]).any(): return ["off"]
    return []
def reference(kids, letter, runs, top, off):
    s = sizes(kids, runs); y = np.zeros((N, 8, Q), np.float32)
    for r in range(N):
        n = gentries(top[r]).astype(np.int64); o = gentries(off[r]).astype(np.int64)
        for h in range(N * LV - 1, -1, -1):
            c, w = parts(kids, s, h, n)
            b = np.sum(o[..., None] >= w[..., 1:], axis=-1)[..., None]
            o = o - np.take_along_axis(w, b, -1)[..., 0]; n = np.take_along_axis(c, b, -1)[..., 0]
        y[r] = letter[0][np.arange(8)[:, None], n]
    return {"y": y}

@@ -1,0 +1,471 @@
+from concourse.bass import DstId, RemoteDMATransfer
+from concourse.mybir import AluOpType as OP
+from concourse.mybir import ActivationFunctionType as AF
+
+NE = 110
+SCRATCH = {
+    "X2": ("sbuf", [128, 64], "int32"), "XT": ("sbuf", [128, 64], "int32"), "U1": ("sbuf", [128, 64], "uint16"),
+    "WIN": ("sbuf", [128, 1024], "int32"), "GS": ("sbuf", [128, 1216], "bfloat16"), "U2": ("sbuf", [128, 128], "uint16"),
+    "U3": ("sbuf", [128, 4, 48], "uint16"),
+    "QI": ("sbuf", [128, 16], "int32"), "SD": ("dram", [4, 128, 16], "int32"),
+    "KQ": ("sbuf", [128, 192], "uint16"), "SY": ("sbuf", [128, 16], "int32"), "AD": ("dram", [4, 128, 8], "float32"),
+    "PX": ("sbuf", [128, 4], "int32"), "FI": ("sbuf", [128, 12], "int32"), "FE": ("sbuf", [128, 12], "float32"),
+    "FD": ("sbuf", [128, 16], "float32"), "SW": ("sbuf", [128, 8], "float32"),
+    "TS": ("sbuf", [128, 20], "float32"), "SEL": ("sbuf", [128, 24], "bfloat16"),
+    "J32": ("sbuf", [128, 32], "float32"), "J1": ("sbuf", [128, 32], "float32"), "MK": ("sbuf", [128, 4], "float32"),
+    "JM": ("sbuf", [128, 96], "float32"), "PE4": ("sbuf", [128, 64], "float32"),
+    "ZM": ("sbuf", [128, 512], "bfloat16"), "A4": ("sbuf", [128, 128], "bfloat16"),
+    "ONE": ("sbuf", [128, 512], "bfloat16"), "IOB": ("sbuf", [128, 512], "bfloat16"), "PUL": ("sbuf", [128, 512], "bfloat16"),
+    "XD": ("sbuf", [128, 512], "bfloat16"), "XM": ("sbuf", [128, 512], "bfloat16"), "EL": ("sbuf", [128, 32], "uint16"),
+    "SELW": ("sbuf", [128, 128], "bfloat16"), "PI": ("sbuf", [128, 128], "bfloat16"), "PC": ("sbuf", [128, 128], "bfloat16"),
+    "I16": ("sbuf", [128, 16], "float32"), "C64": ("sbuf", [128, 64], "float32"), "R64": ("sbuf", [128, 64], "float32"),
+    "QLS": ("sbuf", [128, 16], "uint16"), "QM": ("sbuf", [128, 128], "float32"),
+    "RH4": ("sbuf", [128, 64], "float32"), "M4": ("sbuf", [128, 64], "float32"),
+    "EX": ("sbuf", [128, 512], "bfloat16"), "LW": ("sbuf", [128, 512], "int32"), "PL": ("sbuf", [128, 48], "int32"),
+    "LG": ("sbuf", [128, 512], "bfloat16"), "T0": ("sbuf", [128, 512], "float32"),
+    "QF": ("sbuf", [128, 64], "float32"), "QG": ("sbuf", [128, 256], "float32"),
+    "CC": ("sbuf", [128, 128], "float32"), "ANS": ("sbuf", [128, 8], "float32"),
+    "psS": ("psum", [128, 512], "float32"), "psQ": ("psum", [128, 512], "float32"),
+}
+for _i in range(6):
+    SCRATCH["pb%d" % _i] = ("psum", [128, 512], "float32")
+for _i in range(5):
+    SCRATCH["W%d" % _i] = ("sbuf", [128, 512], "float32")
+for _i in range(4):
+    SCRATCH["NU%d" % _i] = ("sbuf", [128, 16], "uint16")
+    SCRATCH["GD%d" % _i] = ("sbuf", [128, 256], "float32")
+    SCRATCH["TT%d" % _i] = ("sbuf", [128, 256], "float32")
+    SCRATCH["G%d" % _i] = ("sbuf", [128, 512], "bfloat16")
+    SCRATCH["O%d" % _i] = ("sbuf", [128, 64], "float32")
+    SCRATCH["R%d" % _i] = ("sbuf", [128, 128], "float32")
+    SCRATCH["TU%d" % _i] = ("sbuf", [128, 32], "float32")
+SEMAPHORES = (["aS", "sent"] + ["a%s%d" % (k, s) for k in "KQA" for s in range(4)] + ["e%d" % i for i in range(NE)])
+
+
+def bits(engines):
+    m = 0
+    for e in engines:
+        m |= 1 << e
+    return m
+
+
+def routes(T, topo, s):
+    src = T.cores[s]
+    direct, far, used = [], [], []
+    for d, dst in enumerate(T.cores):
+        if d == s:
+            continue
+        if topo.may_write(src, dst):
+            direct.append(d)
+            continue
+        cand = [c for c in topo.cores_of(src) if T.rank_of(c) is None and c not in used and topo.may_write(c, dst)]
+        cand.sort(key=lambda c: topo.die(c) != topo.die(src))
+        used.append(cand[0])
+        far.append((d, cand[0]))
+    return direct, far
+
+
+def hop1_engines(T, topo, s, i):
+    far = routes(T, topo, s)[1]
+    e = topo.engines(T.cores[s], far[i][1])
+    n = len(e) // len(far)
+    return e[i * n:(i + 1) * n]
+
+
+def arrival(T, topo, s, d):
+    last = dict(routes(T, topo, s)[1]).get(d, T.cores[s])
+    return len(topo.engines(last, T.cores[d]))
+
+
+def messages(s):
+    return "SKA" if s == 0 else "QKA"
+
+
+def kcol(s):
+    return 0 if s == 0 else 64 + 32 * s
+
+
+def place(T, kind, s):
+    if kind == "S":
+        return T.SD[0], T.SY[:], T.sem.aS
+    if kind == "K":
+        ap = T.KQ[:, kcol(s):kcol(s) + (48 if s == 0 else 32)]
+        return ap, ap, T.sem["aK%d" % s]
+    if kind == "Q":
+        ap = T.KQ[:, 32 + 16 * s:48 + 16 * s]
+        return ap, ap, T.sem["aQ%d" % s]
+    return T.AD[s], T.AD[s], T.sem["aA%d" % s]
+
+
+def relay_program(g, core, T, topo):
+    for s in range(len(T.cores)):
+        for i, (d, rc) in enumerate(routes(T, topo, s)[1]):
+            if rc != core:
+                continue
+            n = len(hop1_engines(T, topo, s, i))
+            rid, pid = topo.addr(T.cores[d], core)
+            m = topo.mask(core, T.cores[d])
+            for kind in messages(s):
+                here, there, sem = place(T, kind, s)
+                g.wait_ge(sem, n)
+                g.remote_dma(there, here, sem, T.sem.sent, pid, rid, m)
+            g.wait_ge(T.sem.sent, len(messages(s)) * len(topo.engines(core, T.cores[d])))
+
+
+def rank_program(g, core, T, topo):
+    r = T.rank_of(core)
+    if r is None:
+        relay_program(g, core, T, topo)
+        return
+    V, S, P, Y = g.vector, g.scalar, g.tensor, g.sync
+    nxt, seen, sent = [0], {"g": [], "V": [], "S": [], "P": [], "Y": []}, [0]
+    Q = {"g": g, "V": V, "S": S, "P": P, "Y": Y}
+
+    def ev(ins, step=1):
+        name = "e%d" % nxt[0]
+        nxt[0] += 1
+        for i in ins:
+            i.then_inc(T.sem[name], step)
+        return (name, step * len(ins))
+
+    def wait(q, *evs):
+        for e in evs:
+            if e is not None and e not in seen[q]:
+                seen[q].append(e)
+                Q[q].wait_ge(T.sem[e[0]], e[1])
+
+    def arr(kind, s):
+        if s == r:
+            return None
+        return ("aS" if kind == "S" else "a%s%d" % (kind, s), arrival(T, topo, s, r))
+
+    direct, far = routes(T, topo, r)
+
+    def send(kind, src_of):
+        mid, ap, sem = place(T, kind, r)
+        tr = []
+        for i, (d, rc) in enumerate(far):
+            e = hop1_engines(T, topo, r, i)
+            rid, pid = topo.addr(rc, core)
+            tr.append(RemoteDMATransfer(dst_ids=[DstId(rid=rid, pnc=pid)], dma_engine_mask=bits(e), remote_sem=sem,
+                                        src=src_of(d), dst=mid))
+            sent[0] += len(e)
+        g.remote_dma_fused(tr, local_sem=T.sem.sent)
+        for d in direct:
+            rid, pid = topo.addr(T.cores[d], core)
+            g.remote_dma(ap, src_of(d), sem, T.sem.sent, pid, rid, topo.mask(core, T.cores[d]))
+            sent[0] += len(topo.engines(core, T.cores[d]))
+
+    def ts(out, in0, s1, s2, op0, op1=None):
+        if op1 is None:
+            return V.tensor_scalar(out, in0, s1, None, op0)
+        return V.tensor_scalar(out, in0, s1, s2, op0, op1)
+
+    def fiota(out, pat, base, cm):
+        return g.iota(out, pat, base, cm, allow_small_or_imprecise_dtypes=True)
+
+    AND, SHR, EQ, MUL, ADD = OP.bitwise_and, OP.arith_shift_right, OP.is_equal, OP.mult, OP.add
+
+    CUT = 704
+    e_winv = ev([V.memset(T.WIN[:, 0:CUT], 0)])
+    e_wing = ev([g.iota(T.WIN[:, CUT:1024], [[0, 1024 - CUT]], 0, 0)])
+    if r == 0:
+        e_sd = ev([Y.dma_start(T.SD[:, 0:64, :], T.letter[:]), S.dma_start(T.SD[:, 64:128, :], T.runs[:])], 16)
+    e_x2 = ev([Y.dma_start(T.X2[:, 0:32], T.kids[0::2, 1024:2048]), S.dma_start(T.X2[:, 32:64], T.kids[1::2, 1024:2048])], 16)
+    if r != 0:
+        e_q = ev([Y.dma_start(T.QI[:, 0:8], T.top[:]), S.dma_start(T.QI[:, 8:16], T.off[:])], 16)
+    wait("Y", e_winv, e_wing)
+    wait("S", e_winv, e_wing)
+    e_win = ev([Y.dma_start(T.WIN[0::16, :], T.kids[:, 0:1024]), S.dma_start(T.WIN[1::16, :], T.kids[:, 1:1025])], 16)
+    e_sy = arr("S", 0)
+    if r == 0:
+        e_q = ev([Y.dma_start(T.QI[:, 0:8], T.top[:]), S.dma_start(T.QI[:, 8:16], T.off[:])], 16)
+        e_sy = ev([Y.dma_start(T.SY[0:64, :], T.letter[0:2, :]), Y.dma_start(T.SY[64:128, :], T.runs[0:2, :])], 16)
+
+    e_px = ev([g.iota(T.PX[:, 0:1], [[0, 1]], 0, 1)])
+    if r == 0:
+        nsel = 17
+        e_ts = ev([fiota(T.TS[:, 0:8], [[32, 4], [1, 2]], 0, -1), fiota(T.TS[:, 8:9], [[0, 1]], 1, 0),
+                   fiota(T.TS[:, 9:17], [[32, 4], [1, 2]], 16, -1)])
+    else:
+        nsel = 16
+        e_ts = ev([fiota(T.TS[:, 0:16], [[16, 2], [1, 2], [32, 4]], 0, -1)])
+    e_j32 = ev([fiota(T.J32[:], [[0, 8], [1, 4]], 0, 0)])
+    e_pad = ev([V.memset(T.GS[:, 0:96], 0.0), V.memset(T.GS[:, 1120:1216], 0.0)])
+    e_one = ev([V.memset(T.ONE[:], 1.0)])
+    wait("V", e_px)
+    p = T.PX[:, 0:1]
+    e_fi = ev([ts(T.FI[:, 0:1], p, 15, None, AND), ts(T.FI[:, 1:2], p, 5, None, SHR), ts(T.FI[:, 2:3], p, 4, 1, SHR, AND),
+               ts(T.FI[:, 3:4], p, 3, None, AND), ts(T.FI[:, 4:5], p, 3, 1, SHR, AND), ts(T.FI[:, 5:6], p, 7, None, AND),
+               ts(T.FI[:, 6:7], p, 31, None, AND), ts(T.FI[:, 7:8], p, 11, None, AND),
+               ts(T.FI[:, 8:9], p, 5, 1, SHR, AND)])
+    wait("V", e_ts)
+    e_sel = ev([ts(T.SEL[:, 0:nsel], T.TS[:, 0:nsel], 0.0, None, EQ)])
+    wait("V", e_fi, e_one)
+    e_fe = ev([V.tensor_copy(T.FE[:, 0:9], T.FI[:, 0:9])])
+    e_iob = ev([V.tensor_tensor_scan(T.IOB[:], T.ONE[:], T.ONE[:], -257.0, MUL, ADD)])
+    f_t, f_blk, f_c, f_r4, f_b3, f_m8, f_x32, f_p11, f_cp = [T.FE[:, i:i + 1] for i in range(9)]
+
+    def pack_queries(places):
+        wait("V", e_q)
+        ins = []
+        for a, b in places:
+            ins += [V.tensor_copy(a, T.QI[:, 0:8]), ts(b, T.QI[:, 8:16], 1.0, None, ADD)]
+        return ev(ins)
+
+    own_q = (T.KQ[:, 32 + 16 * r:40 + 16 * r], T.KQ[:, 40 + 16 * r:48 + 16 * r])
+    if r == 0:
+        wait("g", e_sd)
+        send("S", lambda d: T.SD[d])
+    else:
+        e_ql = pack_queries([own_q])
+        wait("g", e_ql)
+        send("Q", lambda d: T.KQ[:, 32 + 16 * r:48 + 16 * r])
+    e_i16 = ev([fiota(T.I16[:], [[8, 2], [0, 2], [2, 4]], 0, 0), fiota(T.C64[:], [[0, 8], [1, 2], [0, 4]], 0, 0),
+                fiota(T.R64[:], [[1, 8], [0, 8]], 0, 0)])
+
+    wait("V", e_x2)
+    e_xt = ev([V.transpose(T.XT[:, 32 * c:32 * c + 32], T.X2[:, c::2]) for c in range(2)])
+    wait("V", e_xt)
+    if r == 0:
+        e_u1 = ev([ts(T.U1[:, 2 * h + c::4], T.XT[:, 32 * c + 16 * h:32 * c + 16 * h + 16], 2.0, None, MUL)
+                   for h in range(2) for c in range(2)])
+    else:
+        e_u1 = ev([ts(T.U1[:, c::2], T.XT[:, 32 * c:32 * c + 32], 2.0, None, MUL) for c in range(2)])
+    wait("V", e_u1, e_win)
+    wait("S", e_u1, e_win)
+    e_gv = ev([ts(T.GS[:, 96:608], T.WIN[:, 0:1024].indirect(T.U1[:, 0:32]), -256.0, None, ADD)])
+    e_gs = ev([S.activation(T.GS[:, 608:1120], T.WIN[:, 0:1024].indirect(T.U1[:, 32:64]), AF.Identity, bias=-256.0)])
+    wait("P", e_sel, e_pad, e_gv)
+    mm = []
+    if r == 0:
+        for k in range(-1, 16):
+            if k == 7:
+                wait("P", e_gs)
+            lhs = T.GS[:, 96 + 64 * k:224 + 64 * k]
+            if k == -1:
+                mm.append(P.matmul(T.psS[:, 143:271:16], lhs, T.SEL[:, 9:17], True, True))
+            elif k == 15:
+                mm.append(P.matmul(T.psS[:, 15:128:16], lhs, T.SEL[:, 0:8], True, True))
+            else:
+                mm.append(P.matmul(T.psS[:, k:k + 272:16], lhs, T.SEL[:, 0:17], True, True))
+    else:
+        for k in range(-3, 32):
+            if k == 0:
+                e_head = ev(mm)
+                mm = []
+            if k == 13:
+                wait("P", e_gs, e_head)
+            n0, n1, m = 4 * max(0, -k), 4 * min(4, 32 - k), 32 * min(4, 32 - k)
+            mm.append(P.matmul(T.psS[0:m, 32 * n0 + k + 3:32 * (n1 - 1) + k + 4:32], T.GS[:, 96 + 32 * k:96 + 32 * k + m],
+                               T.SEL[:, n0:n1], True, True))
+    e_mm = ev(mm)
+    if r == 0:
+        e_ql = pack_queries([(T.U3[:, d, 32:40], T.U3[:, d, 40:48]) for d in range(1, 4)] + [own_q])
+    e_pul0 = ev([V.memset(T.PUL[:], 0.0)])
+    wait("V", e_pul0)
+    e_pul = ev([V.memset(T.PUL[:, 0::16], 1.0)])
+    wait("V", e_mm)
+    if r == 0:
+        e_u2 = ev([ts(T.U3[0:64, :, 0:32], T.psS[0:64, 0:128], 256.0, None, ADD),
+                   ts(T.U3[64:128, :, 0:32], T.psS[64:128, 143:271], 256.0, None, ADD)])
+        wait("g", e_ql, e_u2)
+        send("K", lambda d: T.U3[:, d, :])
+    else:
+        e_u2 = ev([ts(T.U2[32 * b:32 * b + 32, :], T.psS[32 * b:32 * b + 32, 127 * b + 3:127 * b + 131], 256.0, None, ADD)
+                   for b in range(4)])
+        wait("g", e_u2)
+        send("K", lambda d: T.U2[:, 32 * d:32 * d + 32])
+
+    def lists(l, a, b):
+        if l != r:
+            return T.KQ[:, kcol(l) + a:kcol(l) + b]
+        return T.U3[:, 0, a:b] if r == 0 else T.U2[:, 32 * r + a:32 * r + b]
+
+    wait("V", e_pul, e_fe, e_j32)
+    e_c1 = ev([V.tensor_tensor_scan(T.XD[:], T.ONE[:], T.PUL[:], -1.0, MUL, ADD),
+               ts(T.MK[:], T.J32[:, 0:4], f_blk, None, EQ),
+               ts(T.J1[:], T.J32[:], 1.0, None, ADD),
+               ts(T.FD[:, 0:1], f_p11, 3.0, None, EQ),
+               ts(T.FD[:, 1:2], f_t, 15.0, 512.0, EQ, MUL),
+               ts(T.FD[:, 2:3], f_t, 11.0, 8192.0, EQ, MUL),
+               ts(T.FD[:, 3:4], f_c, 2.0, None, MUL),
+               ts(T.FD[:, 4:5], f_c, 2.0, 1.0, MUL, ADD),
+               ts(T.FD[:, 5:6], f_blk, 2.0, None, OP.is_ge),
+               ts(T.FD[:, 6:7], f_r4, 16.0, f_b3, MUL, ADD),
+               ts(T.FD[:, 7:8], f_c, 2.0, f_b3, MUL, ADD),
+               ts(T.FD[:, 8:9], f_c, 2.0, f_cp, MUL, ADD),
+               ts(T.FD[:, 9:10], f_blk, 2.0, None, OP.is_lt),
+               ts(T.FD[:, 10:11], f_t, 0.0, None, EQ),
+               ts(T.FD[:, 11:12], f_t, 1.0, 256.0, EQ, MUL),
+               ts(T.FD[:, 12:13], f_t, 2.0, 65536.0, EQ, MUL),
+               ts(T.EL[:], T.ONE[:, 0:32], f_t, None, MUL),
+               V.memset(T.SELW[:], 0.0), V.memset(T.PI[:], 0.0), V.memset(T.PC[:], 0.0), V.memset(T.CC[:], 1.0)])
+    e_lw0 = ev([V.memset(T.LW[:], 0)])
+    wait("V", e_c1)
+    d_a37, d_512, d_iw, d_k0, d_k1, d_hi, d_ql, d_code, d_k4, d_lo, d_l0, d_l1, d_l2 = [T.FD[:, i:i + 1] for i in range(13)]
+    c2 = [ts(T.XM[:], T.XD[:], f_x32, d_hi, EQ, MUL),
+          ts(T.SW[:, 0:1], d_a37, d_512, None, ADD), ts(T.SW[:, 1:2], d_code, -2.0, None, ADD),
+          ts(T.SW[:, 2:3], d_l0, d_l1, d_l2, ADD, ADD),
+          ts(T.SELW[:, 3:64:16], T.ONE[:, 0:4], T.MK[:, 2:3], None, MUL),
+          ts(T.SELW[:, 67:128:16], T.ONE[:, 0:4], T.MK[:, 3:4], None, MUL),
+          V.memset(T.PI[:, 11::16], 1.0), V.memset(T.PC[:, 3::16], -256.0), V.memset(T.PC[:, 7::16], -256.0),
+          V.memset(T.PC[:, 15::16], 1.0)]
+    c2 += [ts(T.JM[:, 32 * H + 16 * y:32 * H + 16 * y + 16], T.J1[:, 16 * y:16 * y + 16],
+              T.MK[:, 2 * y + H:2 * y + H + 1], -1.0, MUL, ADD) for H in range(2) for y in range(2)]
+    c2 += [ts(T.JM[:, 64 + 16 * y:80 + 16 * y], T.J1[:, 16 * y:16 * y + 16], (d_lo, d_hi)[y], -1.0, MUL, ADD) for y in range(2)]
+    e_c2 = ev(c2)
+    wait("V", e_c2)
+    sw, lw, nlw = T.SW[:, 0:1], T.SW[:, 2:3], T.SW[:, 3:4]
+    e_nlw = ev([ts(nlw, lw, -1.0, None, MUL)])
+    jm4 = T.JM[:, 64:96]
+    e_a1 = ev([ts(T.PE4[:, 0:32], jm4, d_k4, sw, OP.is_gt, MUL), ts(T.PE4[:, 32:64], jm4, d_k4, d_iw, EQ, MUL)])
+    a1 = [ts(T.A4[:, 1::4], jm4, d_k4, sw, OP.is_gt, MUL), ts(T.A4[:, 3::4], jm4, f_c, d_a37, EQ, MUL)]
+    for H in range(2):
+        for c in range(2):
+            a = 2 * H + c
+            jm, kk = T.JM[:, 32 * H:32 * H + 32], (d_k0, d_k1)[c]
+            a1 += [ts(T.ZM[:, 128 * a + 1:128 * a + 128:4], jm, kk, sw, OP.is_gt, MUL),
+                   ts(T.ZM[:, 128 * a + 2:128 * a + 128:4], jm, kk, lw, EQ, MUL),
+                   ts(T.ZM[:, 128 * a + 3:128 * a + 128:4], jm, f_c, d_a37, EQ, MUL)]
+    wait("V", e_nlw, e_a1)
+    for H in range(2):
+        for c in range(2):
+            a = 2 * H + c
+            a1.append(ts(T.ZM[:, 128 * a:128 * a + 128:4], T.JM[:, 32 * H:32 * H + 32], (d_k0, d_k1)[c], nlw, EQ, MUL))
+    a1 += [V.tensor_tensor(T.A4[:, 2::4], T.PE4[:, 32:64], T.PE4[:, 0:32], OP.subtract),
+           V.tensor_tensor(T.A4[:, 0::4], T.PE4[:, 0:32], T.PE4[:, 32:64], OP.subtract)]
+    e_am = ev(a1)
+    wait("V", e_i16)
+    e_qc = ev([ts(T.QLS[:], T.I16[:], d_ql, None, ADD),
+               ts(T.QM[:, 0:64], T.C64[:], d_code, T.MK[:, r:r + 1], EQ, MUL),
+               ts(T.QM[:, 64:128], T.C64[:], T.SW[:, 1:2], T.MK[:, r:r + 1], EQ, MUL),
+               ts(T.RH4[:], T.R64[:], f_m8, None, EQ), ts(T.M4[:], T.C64[:], f_c, None, EQ)])
+
+    banks = [(T.pb0, T.pb1), (T.pb2, T.pb3), (T.pb4, T.pb5), (T.pb0, T.pb1), (T.pb2, T.pb3)]
+
+    def open_window(w):
+        for H in range(2):
+            P.matmul(banks[w][H][:, 0:256], T.PI[0:1, :], T.IOB[0:1, 256 * H:256 * H + 256], True, False)
+            if w == 3:
+                P.matmul(banks[w][H][:, 0:256], T.PC[0:1, :], T.ONE[0:1, 0:256], False, False)
+
+    def close_window(w, e0, e1):
+        W = T["W%d" % w]
+        wait("V", e0)
+        ev0 = ev([V.tensor_copy(W[:, 0:256], banks[w][0][:, 0:256])])
+        wait("S", e1)
+        ev1 = ev([S.activation(W[:, 256:512], banks[w][1][:, 0:256], AF.Identity)])
+        return ev0, ev1
+
+    wait("P", e_c2, e_iob, e_one)
+    for w in range(3):
+        open_window(w)
+    wait("V", e_sy)
+    ex = [ev([V.tensor_tensor(T.EX[:, 256 * H:256 * H + 256], T.SY[:, 0:16].indirect(T.EL[:, 16 * H:16 * H + 16]),
+                              T.XM[:, 256 * H:256 * H + 256], MUL)]) for H in range(2)]
+    em = []
+    for H in range(2):
+        wait("P", ex[H])
+        em.append(ev([P.matmul(banks[0][H][:, 0:256], T.SELW[:], T.EX[:, 256 * H:256 * H + 256], False, True)]))
+    ew = close_window(0, em[0], em[1])
+    e_pl = ev([ts(T.PL[0:64, 0:16], T.SY[0:64, :], 255, None, AND), ts(T.PL[0:64, 16:32], T.SY[0:64, :], 8, 255, SHR, AND),
+               ts(T.PL[0:64, 32:48], T.SY[0:64, :], 16, None, SHR)])
+    wait("Y", e_pl, e_lw0)
+    e_lw = ev([Y.dma_start(T.LW[16 * q + j::64, :], T.PL[0:64, 16 * j:16 * j + 16]) for q in range(4) for j in range(3)], 16)
+
+    wait("P", e_am)
+    for l in range(4):
+        W, G = T["W%d" % l], T["G%d" % l]
+        ek = e_u2 if l == r else arr("K", l)
+        wait("V", ek, *ew)
+        wait("S", ek, *ew)
+        e0 = ev([V.tensor_copy(G[:, 0:256], W[:, 0:512].indirect(lists(l, 0, 16)))])
+        e1 = ev([S.activation(G[:, 256:512], W[:, 0:512].indirect(lists(l, 16, 32)), AF.Identity)])
+        if l == 0:
+            wait("V", e_ql, e_qc, *[arr("Q", s) for s in range(1, 4)])
+            e_qf = ev([V.tensor_copy(T.QF[:], T.KQ[:, 32:96])])
+            wait("V", e_qf)
+            e_qt = ev([V.tensor_tensor(T.QG[:, 0:128], T.QF[:, 0:64].indirect(T.QLS[:, 0:8]), T.QM[:], MUL)])
+        if l == 1:
+            e_qo = ev([V.tensor_tensor(T.QG[:, 128:256], T.QF[:, 0:64].indirect(T.QLS[:, 8:16]), T.QM[:], MUL)])
+        if l == 2:
+            wait("V", e_qm)
+            e_nu = ev([V.tensor_copy(T.NU0[:], T.psQ[:, 0:16])])
+            e_o = ev([V.tensor_tensor(T.O0[:], T.psQ[:, 64:128], T.M4[:], MUL)])
+        em = []
+        for H in range(2):
+            out = banks[l + 1][H][:, 0:256]
+            if l == 0:
+                wait("P", e0, e1)
+                P.matmul(out, T.ZM[:, 256 * H:256 * H + 128], G[:, 0:256], False, False)
+                em.append(ev([P.matmul(out, T.ZM[:, 256 * H + 128:256 * H + 256], G[:, 256:512], False, True)]))
+            else:
+                wait("P", (e0, e1)[H])
+                em.append(ev([P.matmul(out, T.A4[:], G[:, 256 * H:256 * H + 256], l == 3, True)]))
+        if l == 1:
+            open_window(3)
+            wait("P", e_qt, e_qo, e_qc)
+            e_qm = ev([P.matmul(T.psQ[:, 0:16], T.QG[:, 0:128], T.RH4[:, 0::4], True, True),
+                       P.matmul(T.psQ[:, 64:128], T.QG[:, 128:256], T.RH4[:], True, True)])
+        ew = close_window(l + 1, em[0], em[1])
+
+    for H in range(2):
+        for c in range(2):
+            P.matmul(banks[2][H][:, 0:256], T.ZM[:, 256 * H + 128 * c:256 * H + 128 * c + 128], T.G0[:, 256 * c:256 * c + 256],
+                     c == 0, False)
+
+    wait("S", *ew)
+    for d in range(4):
+        W, NU, GD, TT = (T.W4, T.W3, T.W2, T.T0)[d], T["NU%d" % d], T["GD%d" % d], T["TT%d" % d]
+        O, R, TU = T["O%d" % d], T["R%d" % d], T["TU%d" % d]
+        wait("S", e_nu)
+        e_gd = ev([S.activation(GD[:], W[:, 0:512].indirect(NU[:, 0:16]), AF.Identity)])
+        if d == 0:
+            wait("S", e_lw)
+            e_lg = [ev([S.activation(T.LG[:, 256 * c:256 * c + 256], T.LW[:, 0:512].indirect(lists(0, 16 * c, 16 * c + 16)),
+                                     AF.Identity)]) for c in range(2)]
+            em = []
+            for c in range(2):
+                wait("P", e_lg[c])
+                for H in range(2):
+                    i = P.matmul(banks[2][H][:, 0:256], T.ZM[:, 256 * H + 128 * c:256 * H + 128 * c + 128],
+                                 T.LG[:, 256 * c:256 * c + 256], False, c == 1)
+                    if c == 1:
+                        em.append(i)
+            e_t0m = ev(em)
+        if d == 2:
+            wait("S", e_t0m)
+            e_t0 = ev([S.activation(T.T0[:, 256 * H:256 * H + 256], banks[2][H][:, 0:256], AF.Identity) for H in range(2)])
+            wait("S", e_t0)
+        wait("V", e_gd)
+        e_tt = ev([V.transpose(TT[:], GD[:])])
+        wait("V", e_tt, e_o)
+        e_cc = ev([V.tensor_tensor(T.CC[:, 1::2], TT[:, 1::4], O[:], OP.is_ge)])
+        wait("V", e_cc)
+        e_r = ev([V.tensor_tensor_scan(R[:], T.CC[:], TT[:, 0::2], 0.0, MUL, ADD)])
+        wait("V", e_r)
+        if d < 3:
+            N2 = T["NU%d" % (d + 1)]
+            e_nu = ev([ts(N2[:], R[:, 7::8], 1.0 / 8192.0, 256.4, MUL, ADD)])
+            e_t = ev([V.tensor_tensor(TU[:, 0:16], R[:, 7::8], O[:, 0::4], ADD)])
+            wait("V", e_nu)
+            e_u = ev([ts(TU[:, 16:32], N2[:], -256.0, -8192.0, ADD, MUL)])
+            wait("V", e_t, e_u)
+            O2 = T["O%d" % (d + 1)]
+            e_o = ev([V.tensor_tensor(O2[:, k::4], TU[:, 0:16], TU[:, 16:32], ADD) for k in range(4)])
+        else:
+            e_ans = ev([V.tensor_copy(T.ANS[:], R[:, 15::16])])
+
+    wait("g", e_ans)
+    send("A", lambda d: T.ANS[:])
+    wait("S", e_ans)
+    st = [S.dma_start(T.y[2 * r:2 * r + 2, :], T.ANS[r::4, :])]
+    order = direct + [d for d, _ in far]
+    for i, d in enumerate(order):
+        q = "YYS"[i]
+        wait(q, arr("A", d))
+        st.append(Q[q].dma_start(T.y[2 * d:2 * d + 2, :], T.AD[d, r::4, :]))
+    e_st = ev(st, 16)
+    wait("Y", e_st)
+    g.wait_ge(T.sem.sent, sent[0])

@@ -2,7 +2,8 @@ from concourse.bass import DstId, RemoteDMATransfer
 from concourse.mybir import AluOpType as OP
 from concourse.mybir import ActivationFunctionType as AF
 
-NE = 110
+NE = 134
+ONE_RELAY_BACK = False
 SCRATCH = {
     "X2": ("sbuf", [128, 64], "int32"), "XT": ("sbuf", [128, 64], "int32"), "U1": ("sbuf", [128, 64], "uint16"),
     "WIN": ("sbuf", [128, 1024], "int32"), "GS": ("sbuf", [128, 1216], "bfloat16"), "U2": ("sbuf", [128, 128], "uint16"),
@@ -12,10 +13,10 @@ SCRATCH = {
     "PX": ("sbuf", [128, 4], "int32"), "FI": ("sbuf", [128, 12], "int32"), "FE": ("sbuf", [128, 12], "float32"),
     "FD": ("sbuf", [128, 16], "float32"), "SW": ("sbuf", [128, 8], "float32"),
     "TS": ("sbuf", [128, 20], "float32"), "SEL": ("sbuf", [128, 24], "bfloat16"),
-    "J32": ("sbuf", [128, 32], "float32"), "J1": ("sbuf", [128, 32], "float32"), "MK": ("sbuf", [128, 4], "float32"),
+    "J1": ("sbuf", [128, 32], "float32"), "MK": ("sbuf", [128, 4], "float32"),
     "JM": ("sbuf", [128, 96], "float32"), "PE4": ("sbuf", [128, 64], "float32"),
     "ZM": ("sbuf", [128, 512], "bfloat16"), "A4": ("sbuf", [128, 128], "bfloat16"),
-    "ONE": ("sbuf", [128, 512], "bfloat16"), "IOB": ("sbuf", [128, 512], "bfloat16"), "PUL": ("sbuf", [128, 512], "bfloat16"),
+    "ONE": ("sbuf", [128, 512], "bfloat16"), "IOB": ("sbuf", [128, 512], "bfloat16"),
     "XD": ("sbuf", [128, 512], "bfloat16"), "XM": ("sbuf", [128, 512], "bfloat16"), "EL": ("sbuf", [128, 32], "uint16"),
     "SELW": ("sbuf", [128, 128], "bfloat16"), "PI": ("sbuf", [128, 128], "bfloat16"), "PC": ("sbuf", [128, 128], "bfloat16"),
     "I16": ("sbuf", [128, 16], "float32"), "C64": ("sbuf", [128, 64], "float32"), "R64": ("sbuf", [128, 64], "float32"),
@@ -49,6 +50,11 @@ def bits(engines):
     return m
 
 
+def share(engines, parts, i):
+    n = len(engines) // parts
+    return engines[i * n:(i + 1) * n]
+
+
 def routes(T, topo, s):
     src = T.cores[s]
     direct, far, used = [], [], []
@@ -65,16 +71,23 @@ def routes(T, topo, s):
     return direct, far
 
 
-def hop1_engines(T, topo, s, i):
+def hops(T, topo, kind, s):
     far = routes(T, topo, s)[1]
-    e = topo.engines(T.cores[s], far[i][1])
-    n = len(e) // len(far)
-    return e[i * n:(i + 1) * n]
+    src = T.cores[s]
+    if kind == "A" and ONE_RELAY_BACK:
+        rc = far[0][1]
+        return [(rc, topo.engines(src, rc),
+                 [(d, share(topo.engines(rc, T.cores[d]), len(far), i)) for i, (d, _) in enumerate(far)])]
+    return [(rc, share(topo.engines(src, rc), len(far), i), [(d, topo.engines(rc, T.cores[d]))])
+            for i, (d, rc) in enumerate(far)]
 
 
-def arrival(T, topo, s, d):
-    last = dict(routes(T, topo, s)[1]).get(d, T.cores[s])
-    return len(topo.engines(last, T.cores[d]))
+def arrival(T, topo, kind, s, d):
+    for _, _, out in hops(T, topo, kind, s):
+        for dd, e in out:
+            if dd == d:
+                return len(e)
+    return len(topo.engines(T.cores[s], T.cores[d]))
 
 
 def messages(s):
@@ -97,19 +110,32 @@ def place(T, kind, s):
     return T.AD[s], T.AD[s], T.sem["aA%d" % s]
 
 
+def write(g, T, topo, core, parts, sem):
+    if len(parts) == 1:
+        dst, e, src, out = parts[0]
+        rid, pid = topo.addr(dst, core)
+        g.remote_dma(out, src, sem, T.sem.sent, pid, rid, bits(e))
+    else:
+        tr = []
+        for dst, e, src, out in parts:
+            rid, pid = topo.addr(dst, core)
+            tr.append(RemoteDMATransfer(dst_ids=[DstId(rid=rid, pnc=pid)], dma_engine_mask=bits(e), remote_sem=sem,
+                                        src=src, dst=out))
+        g.remote_dma_fused(tr, local_sem=T.sem.sent)
+    return sum(len(x[1]) for x in parts)
+
+
 def relay_program(g, core, T, topo):
+    sent = 0
     for s in range(len(T.cores)):
-        for i, (d, rc) in enumerate(routes(T, topo, s)[1]):
-            if rc != core:
-                continue
-            n = len(hop1_engines(T, topo, s, i))
-            rid, pid = topo.addr(T.cores[d], core)
-            m = topo.mask(core, T.cores[d])
-            for kind in messages(s):
-                here, there, sem = place(T, kind, s)
-                g.wait_ge(sem, n)
-                g.remote_dma(there, here, sem, T.sem.sent, pid, rid, m)
-            g.wait_ge(T.sem.sent, len(messages(s)) * len(topo.engines(core, T.cores[d])))
+        for kind in messages(s):
+            for rc, e, out in hops(T, topo, kind, s):
+                if rc == core:
+                    here, there, sem = place(T, kind, s)
+                    g.wait_ge(sem, len(e))
+                    sent += write(g, T, topo, core, [(T.cores[d], ee, here, there) for d, ee in out], sem)
+    if sent:
+        g.wait_ge(T.sem.sent, sent)
 
 
 def rank_program(g, core, T, topo):
@@ -137,29 +163,23 @@ def rank_program(g, core, T, topo):
     def arr(kind, s):
         if s == r:
             return None
-        return ("aS" if kind == "S" else "a%s%d" % (kind, s), arrival(T, topo, s, r))
+        return ("aS" if kind == "S" else "a%s%d" % (kind, s), arrival(T, topo, kind, s, r))
 
     direct, far = routes(T, topo, r)
 
     def send(kind, src_of):
         mid, ap, sem = place(T, kind, r)
-        tr = []
-        for i, (d, rc) in enumerate(far):
-            e = hop1_engines(T, topo, r, i)
-            rid, pid = topo.addr(rc, core)
-            tr.append(RemoteDMATransfer(dst_ids=[DstId(rid=rid, pnc=pid)], dma_engine_mask=bits(e), remote_sem=sem,
-                                        src=src_of(d), dst=mid))
-            sent[0] += len(e)
-        g.remote_dma_fused(tr, local_sem=T.sem.sent)
+        sent[0] += write(g, T, topo, core, [(rc, e, src_of(out[0][0]), mid) for rc, e, out in hops(T, topo, kind, r)], sem)
         for d in direct:
-            rid, pid = topo.addr(T.cores[d], core)
-            g.remote_dma(ap, src_of(d), sem, T.sem.sent, pid, rid, topo.mask(core, T.cores[d]))
-            sent[0] += len(topo.engines(core, T.cores[d]))
+            sent[0] += write(g, T, topo, core, [(T.cores[d], topo.engines(core, T.cores[d]), src_of(d), ap)], sem)
 
     def ts(out, in0, s1, s2, op0, op1=None):
         if op1 is None:
             return V.tensor_scalar(out, in0, s1, None, op0)
         return V.tensor_scalar(out, in0, s1, s2, op0, op1)
+
+    def act(out, in_, scale=1.0, bias=0.0, func=AF.Identity):
+        return S.activation(out, in_, func, bias=bias, scale=scale)
 
     def fiota(out, pat, base, cm):
         return g.iota(out, pat, base, cm, allow_small_or_imprecise_dtypes=True)
@@ -172,14 +192,12 @@ def rank_program(g, core, T, topo):
     if r == 0:
         e_sd = ev([Y.dma_start(T.SD[:, 0:64, :], T.letter[:]), S.dma_start(T.SD[:, 64:128, :], T.runs[:])], 16)
     e_x2 = ev([Y.dma_start(T.X2[:, 0:32], T.kids[0::2, 1024:2048]), S.dma_start(T.X2[:, 32:64], T.kids[1::2, 1024:2048])], 16)
-    if r != 0:
-        e_q = ev([Y.dma_start(T.QI[:, 0:8], T.top[:]), S.dma_start(T.QI[:, 8:16], T.off[:])], 16)
+    e_q = ev([Y.dma_start(T.QI[:, 0:8], T.top[:]), S.dma_start(T.QI[:, 8:16], T.off[:])], 16)
     wait("Y", e_winv, e_wing)
     wait("S", e_winv, e_wing)
     e_win = ev([Y.dma_start(T.WIN[0::16, :], T.kids[:, 0:1024]), S.dma_start(T.WIN[1::16, :], T.kids[:, 1:1025])], 16)
     e_sy = arr("S", 0)
     if r == 0:
-        e_q = ev([Y.dma_start(T.QI[:, 0:8], T.top[:]), S.dma_start(T.QI[:, 8:16], T.off[:])], 16)
         e_sy = ev([Y.dma_start(T.SY[0:64, :], T.letter[0:2, :]), Y.dma_start(T.SY[64:128, :], T.runs[0:2, :])], 16)
 
     e_px = ev([g.iota(T.PX[:, 0:1], [[0, 1]], 0, 1)])
@@ -190,9 +208,9 @@ def rank_program(g, core, T, topo):
     else:
         nsel = 16
         e_ts = ev([fiota(T.TS[:, 0:16], [[16, 2], [1, 2], [32, 4]], 0, -1)])
-    e_j32 = ev([fiota(T.J32[:], [[0, 8], [1, 4]], 0, 0)])
-    e_pad = ev([V.memset(T.GS[:, 0:96], 0.0), V.memset(T.GS[:, 1120:1216], 0.0)])
+    e_j1 = ev([fiota(T.J1[:], [[0, 8], [1, 4]], 1, 0)])
     e_one = ev([V.memset(T.ONE[:], 1.0)])
+    e_pad = ev([V.memset(T.GS[:, 0:96], 0.0), V.memset(T.GS[:, 1120:1216], 0.0)])
     wait("V", e_px)
     p = T.PX[:, 0:1]
     e_fi = ev([ts(T.FI[:, 0:1], p, 15, None, AND), ts(T.FI[:, 1:2], p, 5, None, SHR), ts(T.FI[:, 2:3], p, 4, 1, SHR, AND),
@@ -205,37 +223,60 @@ def rank_program(g, core, T, topo):
     e_fe = ev([V.tensor_copy(T.FE[:, 0:9], T.FI[:, 0:9])])
     e_iob = ev([V.tensor_tensor_scan(T.IOB[:], T.ONE[:], T.ONE[:], -257.0, MUL, ADD)])
     f_t, f_blk, f_c, f_r4, f_b3, f_m8, f_x32, f_p11, f_cp = [T.FE[:, i:i + 1] for i in range(9)]
+    wait("S", e_one)
+    e_zero = ev([act(b[:], T.ONE[:, 0:128], 0.0) for b in (T.SELW, T.PI, T.PC)])
 
-    def pack_queries(places):
+    def pack_queries():
         wait("V", e_q)
-        ins = []
-        for a, b in places:
-            ins += [V.tensor_copy(a, T.QI[:, 0:8]), ts(b, T.QI[:, 8:16], 1.0, None, ADD)]
-        return ev(ins)
+        return ev([V.tensor_copy(T.KQ[:, 32 + 16 * r:40 + 16 * r], T.QI[:, 0:8]),
+                   ts(T.KQ[:, 40 + 16 * r:48 + 16 * r], T.QI[:, 8:16], 1.0, None, ADD)])
 
-    own_q = (T.KQ[:, 32 + 16 * r:40 + 16 * r], T.KQ[:, 40 + 16 * r:48 + 16 * r])
+    own_q = T.KQ[:, 32 + 16 * r:48 + 16 * r]
     if r == 0:
         wait("g", e_sd)
         send("S", lambda d: T.SD[d])
     else:
-        e_ql = pack_queries([own_q])
+        e_ql = pack_queries()
         wait("g", e_ql)
-        send("Q", lambda d: T.KQ[:, 32 + 16 * r:48 + 16 * r])
+        send("Q", lambda d: own_q)
     e_i16 = ev([fiota(T.I16[:], [[8, 2], [0, 2], [2, 4]], 0, 0), fiota(T.C64[:], [[0, 8], [1, 2], [0, 4]], 0, 0),
                 fiota(T.R64[:], [[1, 8], [0, 8]], 0, 0)])
 
+    def small_constants():
+        wait("V", e_fe, e_j1)
+        return ev([ts(T.FD[:, 13:14], f_x32, -16.0, 248.5, MUL, ADD),
+                   ts(T.MK[:], T.J1[:, 0:4], -1.0, f_blk, ADD, EQ),
+                   ts(T.FD[:, 0:1], f_p11, 3.0, None, EQ),
+                   ts(T.FD[:, 1:2], f_t, 15.0, 512.0, EQ, MUL),
+                   ts(T.FD[:, 2:3], f_t, 11.0, 8192.0, EQ, MUL),
+                   ts(T.FD[:, 3:4], f_c, 2.0, None, MUL),
+                   ts(T.FD[:, 4:5], f_c, 2.0, 1.0, MUL, ADD),
+                   ts(T.FD[:, 5:6], f_blk, 2.0, None, OP.is_ge),
+                   ts(T.FD[:, 6:7], f_r4, 16.0, f_b3, MUL, ADD),
+                   ts(T.FD[:, 7:8], f_c, 2.0, f_b3, MUL, ADD),
+                   ts(T.FD[:, 8:9], f_c, 2.0, f_cp, MUL, ADD),
+                   ts(T.FD[:, 9:10], f_blk, 2.0, None, OP.is_lt),
+                   ts(T.FD[:, 10:11], f_t, 0.0, None, EQ),
+                   ts(T.FD[:, 11:12], f_t, 1.0, 256.0, EQ, MUL),
+                   ts(T.FD[:, 12:13], f_t, 2.0, 65536.0, EQ, MUL),
+                   ts(T.EL[:], T.ONE[:, 0:32], f_t, None, MUL)])
+
     wait("V", e_x2)
     e_xt = ev([V.transpose(T.XT[:, 32 * c:32 * c + 32], T.X2[:, c::2]) for c in range(2)])
+    if r == 0:
+        e_ql = pack_queries()
     wait("V", e_xt)
     if r == 0:
         e_u1 = ev([ts(T.U1[:, 2 * h + c::4], T.XT[:, 32 * c + 16 * h:32 * c + 16 * h + 16], 2.0, None, MUL)
                    for h in range(2) for c in range(2)])
+        wait("V", e_ql)
+        e_q3 = ev([V.tensor_copy(T.U3[:, d, 32:48], own_q) for d in range(1, 4)])
     else:
         e_u1 = ev([ts(T.U1[:, c::2], T.XT[:, 32 * c:32 * c + 32], 2.0, None, MUL) for c in range(2)])
     wait("V", e_u1, e_win)
     wait("S", e_u1, e_win)
     e_gv = ev([ts(T.GS[:, 96:608], T.WIN[:, 0:1024].indirect(T.U1[:, 0:32]), -256.0, None, ADD)])
-    e_gs = ev([S.activation(T.GS[:, 608:1120], T.WIN[:, 0:1024].indirect(T.U1[:, 32:64]), AF.Identity, bias=-256.0)])
+    e_gs = ev([act(T.GS[:, 608:1120], T.WIN[:, 0:1024].indirect(T.U1[:, 32:64]), bias=-256.0)])
     wait("P", e_sel, e_pad, e_gv)
     mm = []
     if r == 0:
@@ -261,86 +302,54 @@ def rank_program(g, core, T, topo):
                                T.SEL[:, n0:n1], True, True))
     e_mm = ev(mm)
     if r == 0:
-        e_ql = pack_queries([(T.U3[:, d, 32:40], T.U3[:, d, 40:48]) for d in range(1, 4)] + [own_q])
-    e_pul0 = ev([V.memset(T.PUL[:], 0.0)])
-    wait("V", e_pul0)
-    e_pul = ev([V.memset(T.PUL[:, 0::16], 1.0)])
-    wait("V", e_mm)
-    if r == 0:
+        wait("V", e_mm)
         e_u2 = ev([ts(T.U3[0:64, :, 0:32], T.psS[0:64, 0:128], 256.0, None, ADD),
                    ts(T.U3[64:128, :, 0:32], T.psS[64:128, 143:271], 256.0, None, ADD)])
-        wait("g", e_ql, e_u2)
+        e_c1 = small_constants()
+        wait("g", e_q3, e_u2)
         send("K", lambda d: T.U3[:, d, :])
     else:
+        e_c1 = small_constants()
+        wait("V", e_mm)
         e_u2 = ev([ts(T.U2[32 * b:32 * b + 32, :], T.psS[32 * b:32 * b + 32, 127 * b + 3:127 * b + 131], 256.0, None, ADD)
                    for b in range(4)])
         wait("g", e_u2)
         send("K", lambda d: T.U2[:, 32 * d:32 * d + 32])
+    e_lw0 = ev([g.iota(T.LW[:], [[0, 512]], 0, 0)])
+    e_cc1 = ev([fiota(T.CC[:], [[0, 128]], 1, 0)])
 
     def lists(l, a, b):
         if l != r:
             return T.KQ[:, kcol(l) + a:kcol(l) + b]
         return T.U3[:, 0, a:b] if r == 0 else T.U2[:, 32 * r + a:32 * r + b]
 
-    wait("V", e_pul, e_fe, e_j32)
-    e_c1 = ev([V.tensor_tensor_scan(T.XD[:], T.ONE[:], T.PUL[:], -1.0, MUL, ADD),
-               ts(T.MK[:], T.J32[:, 0:4], f_blk, None, EQ),
-               ts(T.J1[:], T.J32[:], 1.0, None, ADD),
-               ts(T.FD[:, 0:1], f_p11, 3.0, None, EQ),
-               ts(T.FD[:, 1:2], f_t, 15.0, 512.0, EQ, MUL),
-               ts(T.FD[:, 2:3], f_t, 11.0, 8192.0, EQ, MUL),
-               ts(T.FD[:, 3:4], f_c, 2.0, None, MUL),
-               ts(T.FD[:, 4:5], f_c, 2.0, 1.0, MUL, ADD),
-               ts(T.FD[:, 5:6], f_blk, 2.0, None, OP.is_ge),
-               ts(T.FD[:, 6:7], f_r4, 16.0, f_b3, MUL, ADD),
-               ts(T.FD[:, 7:8], f_c, 2.0, f_b3, MUL, ADD),
-               ts(T.FD[:, 8:9], f_c, 2.0, f_cp, MUL, ADD),
-               ts(T.FD[:, 9:10], f_blk, 2.0, None, OP.is_lt),
-               ts(T.FD[:, 10:11], f_t, 0.0, None, EQ),
-               ts(T.FD[:, 11:12], f_t, 1.0, 256.0, EQ, MUL),
-               ts(T.FD[:, 12:13], f_t, 2.0, 65536.0, EQ, MUL),
-               ts(T.EL[:], T.ONE[:, 0:32], f_t, None, MUL),
-               V.memset(T.SELW[:], 0.0), V.memset(T.PI[:], 0.0), V.memset(T.PC[:], 0.0), V.memset(T.CC[:], 1.0)])
-    e_lw0 = ev([V.memset(T.LW[:], 0)])
+    d_a37, d_512, d_iw, d_k0, d_k1, d_hi, d_ql, d_code, d_k4, d_lo, d_l0, d_l1, d_l2, d_mid = [T.FD[:, i:i + 1] for i in range(14)]
+    wait("S", e_c1, e_iob, e_zero)
+    e_xd = ev([act(T.XD[:], T.IOB[:], bias=d_mid, func=AF.Abs)])
+    e_jm = ev([act(T.JM[:, 32 * H + 16 * y:32 * H + 16 * y + 16], T.J1[:, 16 * y:16 * y + 16],
+                   T.MK[:, 2 * y + H:2 * y + H + 1], -1.0) for H in range(2) for y in range(2)])
+    e_c2 = ev([act(T.SELW[:, 3:64:16], T.ONE[:, 0:4], T.MK[:, 2:3]), act(T.SELW[:, 67:128:16], T.ONE[:, 0:4], T.MK[:, 3:4]),
+               act(T.PI[:, 11::16], T.ONE[:, 0:8]), act(T.PC[:, 3::16], T.ONE[:, 0:8], -256.0),
+               act(T.PC[:, 7::16], T.ONE[:, 0:8], -256.0), act(T.PC[:, 15::16], T.ONE[:, 0:8])])
+    e_jm4 = ev([act(T.JM[:, 64 + 16 * y:80 + 16 * y], T.J1[:, 16 * y:16 * y + 16], (d_lo, d_hi)[y], -1.0) for y in range(2)])
     wait("V", e_c1)
-    d_a37, d_512, d_iw, d_k0, d_k1, d_hi, d_ql, d_code, d_k4, d_lo, d_l0, d_l1, d_l2 = [T.FD[:, i:i + 1] for i in range(13)]
-    c2 = [ts(T.XM[:], T.XD[:], f_x32, d_hi, EQ, MUL),
-          ts(T.SW[:, 0:1], d_a37, d_512, None, ADD), ts(T.SW[:, 1:2], d_code, -2.0, None, ADD),
-          ts(T.SW[:, 2:3], d_l0, d_l1, d_l2, ADD, ADD),
-          ts(T.SELW[:, 3:64:16], T.ONE[:, 0:4], T.MK[:, 2:3], None, MUL),
-          ts(T.SELW[:, 67:128:16], T.ONE[:, 0:4], T.MK[:, 3:4], None, MUL),
-          V.memset(T.PI[:, 11::16], 1.0), V.memset(T.PC[:, 3::16], -256.0), V.memset(T.PC[:, 7::16], -256.0),
-          V.memset(T.PC[:, 15::16], 1.0)]
-    c2 += [ts(T.JM[:, 32 * H + 16 * y:32 * H + 16 * y + 16], T.J1[:, 16 * y:16 * y + 16],
-              T.MK[:, 2 * y + H:2 * y + H + 1], -1.0, MUL, ADD) for H in range(2) for y in range(2)]
-    c2 += [ts(T.JM[:, 64 + 16 * y:80 + 16 * y], T.J1[:, 16 * y:16 * y + 16], (d_lo, d_hi)[y], -1.0, MUL, ADD) for y in range(2)]
-    e_c2 = ev(c2)
-    wait("V", e_c2)
-    sw, lw, nlw = T.SW[:, 0:1], T.SW[:, 2:3], T.SW[:, 3:4]
-    e_nlw = ev([ts(nlw, lw, -1.0, None, MUL)])
-    jm4 = T.JM[:, 64:96]
-    e_a1 = ev([ts(T.PE4[:, 0:32], jm4, d_k4, sw, OP.is_gt, MUL), ts(T.PE4[:, 32:64], jm4, d_k4, d_iw, EQ, MUL)])
-    a1 = [ts(T.A4[:, 1::4], jm4, d_k4, sw, OP.is_gt, MUL), ts(T.A4[:, 3::4], jm4, f_c, d_a37, EQ, MUL)]
-    for H in range(2):
-        for c in range(2):
-            a = 2 * H + c
-            jm, kk = T.JM[:, 32 * H:32 * H + 32], (d_k0, d_k1)[c]
-            a1 += [ts(T.ZM[:, 128 * a + 1:128 * a + 128:4], jm, kk, sw, OP.is_gt, MUL),
-                   ts(T.ZM[:, 128 * a + 2:128 * a + 128:4], jm, kk, lw, EQ, MUL),
-                   ts(T.ZM[:, 128 * a + 3:128 * a + 128:4], jm, f_c, d_a37, EQ, MUL)]
-    wait("V", e_nlw, e_a1)
-    for H in range(2):
-        for c in range(2):
-            a = 2 * H + c
-            a1.append(ts(T.ZM[:, 128 * a:128 * a + 128:4], T.JM[:, 32 * H:32 * H + 32], (d_k0, d_k1)[c], nlw, EQ, MUL))
-    a1 += [V.tensor_tensor(T.A4[:, 2::4], T.PE4[:, 32:64], T.PE4[:, 0:32], OP.subtract),
-           V.tensor_tensor(T.A4[:, 0::4], T.PE4[:, 0:32], T.PE4[:, 32:64], OP.subtract)]
-    e_am = ev(a1)
-    wait("V", e_i16)
-    e_qc = ev([ts(T.QLS[:], T.I16[:], d_ql, None, ADD),
-               ts(T.QM[:, 0:64], T.C64[:], d_code, T.MK[:, r:r + 1], EQ, MUL),
-               ts(T.QM[:, 64:128], T.C64[:], T.SW[:, 1:2], T.MK[:, r:r + 1], EQ, MUL),
-               ts(T.RH4[:], T.R64[:], f_m8, None, EQ), ts(T.M4[:], T.C64[:], f_c, None, EQ)])
+    e_sw = ev([ts(T.SW[:, 0:1], d_a37, d_512, None, ADD), ts(T.SW[:, 1:2], d_code, -2.0, None, ADD),
+               ts(T.SW[:, 2:3], d_l0, d_l1, d_l2, ADD, ADD)])
+    sw, lw = T.SW[:, 0:1], T.SW[:, 2:3]
+    wait("V", e_xd)
+    e_xm = ev([ts(T.XM[:], T.XD[:], 8.0, d_hi, OP.is_lt, MUL)])
+    wait("V", e_sw, e_jm)
+    jm = T.JM[:, 0:64]
+    e_zv = ev([ts(T.ZM[:, 256 * c + 2:256 * c + 256:4], jm, (d_k0, d_k1)[c], lw, EQ, MUL) for c in range(2)])
+    z = []
+    for c in range(2):
+        z += [ts(T.ZM[:, 256 * c + 1:256 * c + 256:4], jm, (d_k0, d_k1)[c], sw, OP.is_gt, MUL),
+              ts(T.ZM[:, 256 * c + 3:256 * c + 256:4], jm, f_c, d_a37, EQ, MUL)]
+    wait("V", e_zv)
+    e_zm = ev(z + [ts(T.ZM[:, 0::4], T.ZM[:, 2::4], -1.0, None, MUL)])
+
+    def zm(H, c):
+        return T.ZM[:, 256 * c + 128 * H:256 * c + 128 * H + 128]
 
     banks = [(T.pb0, T.pb1), (T.pb2, T.pb3), (T.pb4, T.pb5), (T.pb0, T.pb1), (T.pb2, T.pb3)]
 
@@ -352,16 +361,20 @@ def rank_program(g, core, T, topo):
 
     def close_window(w, e0, e1):
         W = T["W%d" % w]
-        wait("V", e0)
-        ev0 = ev([V.tensor_copy(W[:, 0:256], banks[w][0][:, 0:256])])
+        if w == 0:
+            wait("S", e0)
+            ev0 = ev([act(W[:, 0:256], banks[w][0][:, 0:256])])
+        else:
+            wait("V", e0)
+            ev0 = ev([V.tensor_copy(W[:, 0:256], banks[w][0][:, 0:256])])
         wait("S", e1)
-        ev1 = ev([S.activation(W[:, 256:512], banks[w][1][:, 0:256], AF.Identity)])
+        ev1 = ev([act(W[:, 256:512], banks[w][1][:, 0:256])])
         return ev0, ev1
 
     wait("P", e_c2, e_iob, e_one)
     for w in range(3):
         open_window(w)
-    wait("V", e_sy)
+    wait("V", e_sy, e_xm)
     ex = [ev([V.tensor_tensor(T.EX[:, 256 * H:256 * H + 256], T.SY[:, 0:16].indirect(T.EL[:, 16 * H:16 * H + 16]),
                               T.XM[:, 256 * H:256 * H + 256], MUL)]) for H in range(2)]
     em = []
@@ -373,24 +386,36 @@ def rank_program(g, core, T, topo):
                ts(T.PL[0:64, 32:48], T.SY[0:64, :], 16, None, SHR)])
     wait("Y", e_pl, e_lw0)
     e_lw = ev([Y.dma_start(T.LW[16 * q + j::64, :], T.PL[0:64, 16 * j:16 * j + 16]) for q in range(4) for j in range(3)], 16)
+    wait("V", e_i16, e_jm4)
+    jm4 = T.JM[:, 64:96]
+    e_a1 = ev([ts(T.PE4[:, 0:32], jm4, d_k4, sw, OP.is_gt, MUL), ts(T.PE4[:, 32:64], jm4, d_k4, d_iw, EQ, MUL)])
+    a1 = [ts(T.A4[:, 1::4], jm4, d_k4, sw, OP.is_gt, MUL), ts(T.A4[:, 3::4], jm4, f_c, d_a37, EQ, MUL)]
+    e_qc = ev([ts(T.QLS[:], T.I16[:], d_ql, None, ADD),
+               ts(T.QM[:, 0:64], T.C64[:], d_code, T.MK[:, r:r + 1], EQ, MUL),
+               ts(T.QM[:, 64:128], T.C64[:], T.SW[:, 1:2], T.MK[:, r:r + 1], EQ, MUL)])
+    wait("V", e_a1)
+    a1 += [V.tensor_tensor(T.A4[:, 2::4], T.PE4[:, 32:64], T.PE4[:, 0:32], OP.subtract),
+           V.tensor_tensor(T.A4[:, 0::4], T.PE4[:, 0:32], T.PE4[:, 32:64], OP.subtract)]
+    e_am = ev(a1)
 
-    wait("P", e_am)
+    wait("P", e_zm)
     for l in range(4):
         W, G = T["W%d" % l], T["G%d" % l]
         ek = e_u2 if l == r else arr("K", l)
         wait("V", ek, *ew)
         wait("S", ek, *ew)
         e0 = ev([V.tensor_copy(G[:, 0:256], W[:, 0:512].indirect(lists(l, 0, 16)))])
-        e1 = ev([S.activation(G[:, 256:512], W[:, 0:512].indirect(lists(l, 16, 32)), AF.Identity)])
+        e1 = ev([act(G[:, 256:512], W[:, 0:512].indirect(lists(l, 16, 32)))])
         if l == 0:
             wait("V", e_ql, e_qc, *[arr("Q", s) for s in range(1, 4)])
             e_qf = ev([V.tensor_copy(T.QF[:], T.KQ[:, 32:96])])
+            e_rh = ev([ts(T.RH4[:], T.R64[:], f_m8, None, EQ), ts(T.M4[:], T.C64[:], f_c, None, EQ)])
             wait("V", e_qf)
             e_qt = ev([V.tensor_tensor(T.QG[:, 0:128], T.QF[:, 0:64].indirect(T.QLS[:, 0:8]), T.QM[:], MUL)])
         if l == 1:
             e_qo = ev([V.tensor_tensor(T.QG[:, 128:256], T.QF[:, 0:64].indirect(T.QLS[:, 8:16]), T.QM[:], MUL)])
         if l == 2:
-            wait("V", e_qm)
+            wait("V", e_qm, e_rh)
             e_nu = ev([V.tensor_copy(T.NU0[:], T.psQ[:, 0:16])])
             e_o = ev([V.tensor_tensor(T.O0[:], T.psQ[:, 64:128], T.M4[:], MUL)])
         em = []
@@ -398,45 +423,44 @@ def rank_program(g, core, T, topo):
             out = banks[l + 1][H][:, 0:256]
             if l == 0:
                 wait("P", e0, e1)
-                P.matmul(out, T.ZM[:, 256 * H:256 * H + 128], G[:, 0:256], False, False)
-                em.append(ev([P.matmul(out, T.ZM[:, 256 * H + 128:256 * H + 256], G[:, 256:512], False, True)]))
+                P.matmul(out, zm(H, 0), G[:, 0:256], False, False)
+                em.append(ev([P.matmul(out, zm(H, 1), G[:, 256:512], False, True)]))
             else:
-                wait("P", (e0, e1)[H])
+                wait("P", e_am, (e0, e1)[H])
                 em.append(ev([P.matmul(out, T.A4[:], G[:, 256 * H:256 * H + 256], l == 3, True)]))
         if l == 1:
             open_window(3)
-            wait("P", e_qt, e_qo, e_qc)
+            wait("P", e_qt, e_qo, e_rh)
             e_qm = ev([P.matmul(T.psQ[:, 0:16], T.QG[:, 0:128], T.RH4[:, 0::4], True, True),
                        P.matmul(T.psQ[:, 64:128], T.QG[:, 128:256], T.RH4[:], True, True)])
         ew = close_window(l + 1, em[0], em[1])
 
     for H in range(2):
         for c in range(2):
-            P.matmul(banks[2][H][:, 0:256], T.ZM[:, 256 * H + 128 * c:256 * H + 128 * c + 128], T.G0[:, 256 * c:256 * c + 256],
-                     c == 0, False)
+            P.matmul(banks[2][H][:, 0:256], zm(H, c), T.G0[:, 256 * c:256 * c + 256], c == 0, False)
 
     wait("S", *ew)
+    wait("V", e_cc1)
     for d in range(4):
         W, NU, GD, TT = (T.W4, T.W3, T.W2, T.T0)[d], T["NU%d" % d], T["GD%d" % d], T["TT%d" % d]
         O, R, TU = T["O%d" % d], T["R%d" % d], T["TU%d" % d]
         wait("S", e_nu)
-        e_gd = ev([S.activation(GD[:], W[:, 0:512].indirect(NU[:, 0:16]), AF.Identity)])
+        e_gd = ev([act(GD[:], W[:, 0:512].indirect(NU[:, 0:16]))])
         if d == 0:
             wait("S", e_lw)
-            e_lg = [ev([S.activation(T.LG[:, 256 * c:256 * c + 256], T.LW[:, 0:512].indirect(lists(0, 16 * c, 16 * c + 16)),
-                                     AF.Identity)]) for c in range(2)]
+            e_lg = [ev([act(T.LG[:, 256 * c:256 * c + 256], T.LW[:, 0:512].indirect(lists(0, 16 * c, 16 * c + 16)))])
+                    for c in range(2)]
             em = []
             for c in range(2):
                 wait("P", e_lg[c])
                 for H in range(2):
-                    i = P.matmul(banks[2][H][:, 0:256], T.ZM[:, 256 * H + 128 * c:256 * H + 128 * c + 128],
-                                 T.LG[:, 256 * c:256 * c + 256], False, c == 1)
+                    i = P.matmul(banks[2][H][:, 0:256], zm(H, c), T.LG[:, 256 * c:256 * c + 256], False, c == 1)
                     if c == 1:
                         em.append(i)
             e_t0m = ev(em)
         if d == 2:
             wait("S", e_t0m)
-            e_t0 = ev([S.activation(T.T0[:, 256 * H:256 * H + 256], banks[2][H][:, 0:256], AF.Identity) for H in range(2)])
+            e_t0 = ev([act(T.T0[:, 256 * H:256 * H + 256], banks[2][H][:, 0:256]) for H in range(2)])
             wait("S", e_t0)
         wait("V", e_gd)
         e_tt = ev([V.transpose(TT[:], GD[:])])

from concourse.bass import DstId, RemoteDMATransfer
from concourse.mybir import AluOpType as OP
from concourse.mybir import ActivationFunctionType as AF

NE = 134
ONE_RELAY_BACK = False
SCRATCH = {
    "X2": ("sbuf", [128, 64], "int32"), "XT": ("sbuf", [128, 64], "int32"), "U1": ("sbuf", [128, 64], "uint16"),
    "WIN": ("sbuf", [128, 1024], "int32"), "GS": ("sbuf", [128, 1216], "bfloat16"), "U2": ("sbuf", [128, 128], "uint16"),
    "U3": ("sbuf", [128, 4, 48], "uint16"),
    "QI": ("sbuf", [128, 16], "int32"), "SD": ("dram", [4, 128, 16], "int32"),
    "KQ": ("sbuf", [128, 192], "uint16"), "SY": ("sbuf", [128, 16], "int32"), "AD": ("dram", [4, 128, 8], "float32"),
    "PX": ("sbuf", [128, 4], "int32"), "FI": ("sbuf", [128, 12], "int32"), "FE": ("sbuf", [128, 12], "float32"),
    "FD": ("sbuf", [128, 16], "float32"), "SW": ("sbuf", [128, 8], "float32"),
    "TS": ("sbuf", [128, 20], "float32"), "SEL": ("sbuf", [128, 24], "bfloat16"),
    "J1": ("sbuf", [128, 32], "float32"), "MK": ("sbuf", [128, 4], "float32"),
    "JM": ("sbuf", [128, 96], "float32"), "PE4": ("sbuf", [128, 64], "float32"),
    "ZM": ("sbuf", [128, 512], "bfloat16"), "A4": ("sbuf", [128, 128], "bfloat16"),
    "ONE": ("sbuf", [128, 512], "bfloat16"), "IOB": ("sbuf", [128, 512], "bfloat16"),
    "XD": ("sbuf", [128, 512], "bfloat16"), "XM": ("sbuf", [128, 512], "bfloat16"), "EL": ("sbuf", [128, 32], "uint16"),
    "SELW": ("sbuf", [128, 128], "bfloat16"), "PI": ("sbuf", [128, 128], "bfloat16"), "PC": ("sbuf", [128, 128], "bfloat16"),
    "I16": ("sbuf", [128, 16], "float32"), "C64": ("sbuf", [128, 64], "float32"), "R64": ("sbuf", [128, 64], "float32"),
    "QLS": ("sbuf", [128, 16], "uint16"), "QM": ("sbuf", [128, 128], "float32"),
    "RH4": ("sbuf", [128, 64], "float32"), "M4": ("sbuf", [128, 64], "float32"),
    "EX": ("sbuf", [128, 512], "bfloat16"), "LW": ("sbuf", [128, 512], "int32"), "PL": ("sbuf", [128, 48], "int32"),
    "LG": ("sbuf", [128, 512], "bfloat16"), "T0": ("sbuf", [128, 512], "float32"),
    "QF": ("sbuf", [128, 64], "float32"), "QG": ("sbuf", [128, 256], "float32"),
    "CC": ("sbuf", [128, 128], "float32"), "ANS": ("sbuf", [128, 8], "float32"),
    "psS": ("psum", [128, 512], "float32"), "psQ": ("psum", [128, 512], "float32"),
}
for _i in range(6):
    SCRATCH["pb%d" % _i] = ("psum", [128, 512], "float32")
for _i in range(5):
    SCRATCH["W%d" % _i] = ("sbuf", [128, 512], "float32")
for _i in range(4):
    SCRATCH["NU%d" % _i] = ("sbuf", [128, 16], "uint16")
    SCRATCH["GD%d" % _i] = ("sbuf", [128, 256], "float32")
    SCRATCH["TT%d" % _i] = ("sbuf", [128, 256], "float32")
    SCRATCH["G%d" % _i] = ("sbuf", [128, 512], "bfloat16")
    SCRATCH["O%d" % _i] = ("sbuf", [128, 64], "float32")
    SCRATCH["R%d" % _i] = ("sbuf", [128, 128], "float32")
    SCRATCH["TU%d" % _i] = ("sbuf", [128, 32], "float32")
SEMAPHORES = (["aS", "sent"] + ["a%s%d" % (k, s) for k in "KQA" for s in range(4)] + ["e%d" % i for i in range(NE)])


def bits(engines):
    m = 0
    for e in engines:
        m |= 1 << e
    return m


def share(engines, parts, i):
    n = len(engines) // parts
    return engines[i * n:(i + 1) * n]


def routes(T, topo, s):
    src = T.cores[s]
    direct, far, used = [], [], []
    for d, dst in enumerate(T.cores):
        if d == s:
            continue
        if topo.may_write(src, dst):
            direct.append(d)
            continue
        cand = [c for c in topo.cores_of(src) if T.rank_of(c) is None and c not in used and topo.may_write(c, dst)]
        cand.sort(key=lambda c: topo.die(c) != topo.die(src))
        used.append(cand[0])
        far.append((d, cand[0]))
    return direct, far


def hops(T, topo, kind, s):
    far = routes(T, topo, s)[1]
    src = T.cores[s]
    if kind == "A" and ONE_RELAY_BACK:
        rc = far[0][1]
        return [(rc, topo.engines(src, rc),
                 [(d, share(topo.engines(rc, T.cores[d]), len(far), i)) for i, (d, _) in enumerate(far)])]
    return [(rc, share(topo.engines(src, rc), len(far), i), [(d, topo.engines(rc, T.cores[d]))])
            for i, (d, rc) in enumerate(far)]


def arrival(T, topo, kind, s, d):
    for _, _, out in hops(T, topo, kind, s):
        for dd, e in out:
            if dd == d:
                return len(e)
    return len(topo.engines(T.cores[s], T.cores[d]))


def messages(s):
    return "SKA" if s == 0 else "QKA"


def kcol(s):
    return 0 if s == 0 else 64 + 32 * s


def place(T, kind, s):
    if kind == "S":
        return T.SD[0], T.SY[:], T.sem.aS
    if kind == "K":
        ap = T.KQ[:, kcol(s):kcol(s) + (48 if s == 0 else 32)]
        return ap, ap, T.sem["aK%d" % s]
    if kind == "Q":
        ap = T.KQ[:, 32 + 16 * s:48 + 16 * s]
        return ap, ap, T.sem["aQ%d" % s]
    return T.AD[s], T.AD[s], T.sem["aA%d" % s]


def write(g, T, topo, core, parts, sem):
    if len(parts) == 1:
        dst, e, src, out = parts[0]
        rid, pid = topo.addr(dst, core)
        g.remote_dma(out, src, sem, T.sem.sent, pid, rid, bits(e))
    else:
        tr = []
        for dst, e, src, out in parts:
            rid, pid = topo.addr(dst, core)
            tr.append(RemoteDMATransfer(dst_ids=[DstId(rid=rid, pnc=pid)], dma_engine_mask=bits(e), remote_sem=sem,
                                        src=src, dst=out))
        g.remote_dma_fused(tr, local_sem=T.sem.sent)
    return sum(len(x[1]) for x in parts)


def relay_program(g, core, T, topo):
    sent = 0
    for s in range(len(T.cores)):
        for kind in messages(s):
            for rc, e, out in hops(T, topo, kind, s):
                if rc == core:
                    here, there, sem = place(T, kind, s)
                    g.wait_ge(sem, len(e))
                    sent += write(g, T, topo, core, [(T.cores[d], ee, here, there) for d, ee in out], sem)
    if sent:
        g.wait_ge(T.sem.sent, sent)


def rank_program(g, core, T, topo):
    r = T.rank_of(core)
    if r is None:
        relay_program(g, core, T, topo)
        return
    V, S, P, Y = g.vector, g.scalar, g.tensor, g.sync
    nxt, seen, sent = [0], {"g": [], "V": [], "S": [], "P": [], "Y": []}, [0]
    Q = {"g": g, "V": V, "S": S, "P": P, "Y": Y}

    def ev(ins, step=1):
        name = "e%d" % nxt[0]
        nxt[0] += 1
        for i in ins:
            i.then_inc(T.sem[name], step)
        return (name, step * len(ins))

    def wait(q, *evs):
        for e in evs:
            if e is not None and e not in seen[q]:
                seen[q].append(e)
                Q[q].wait_ge(T.sem[e[0]], e[1])

    def arr(kind, s):
        if s == r:
            return None
        return ("aS" if kind == "S" else "a%s%d" % (kind, s), arrival(T, topo, kind, s, r))

    direct, far = routes(T, topo, r)

    def send(kind, src_of):
        mid, ap, sem = place(T, kind, r)
        sent[0] += write(g, T, topo, core, [(rc, e, src_of(out[0][0]), mid) for rc, e, out in hops(T, topo, kind, r)], sem)
        for d in direct:
            sent[0] += write(g, T, topo, core, [(T.cores[d], topo.engines(core, T.cores[d]), src_of(d), ap)], sem)

    def ts(out, in0, s1, s2, op0, op1=None):
        if op1 is None:
            return V.tensor_scalar(out, in0, s1, None, op0)
        return V.tensor_scalar(out, in0, s1, s2, op0, op1)

    def act(out, in_, scale=1.0, bias=0.0, func=AF.Identity):
        return S.activation(out, in_, func, bias=bias, scale=scale)

    def fiota(out, pat, base, cm):
        return g.iota(out, pat, base, cm, allow_small_or_imprecise_dtypes=True)

    AND, SHR, EQ, MUL, ADD = OP.bitwise_and, OP.arith_shift_right, OP.is_equal, OP.mult, OP.add

    CUT = 704
    e_winv = ev([V.memset(T.WIN[:, 0:CUT], 0)])
    e_wing = ev([g.iota(T.WIN[:, CUT:1024], [[0, 1024 - CUT]], 0, 0)])
    if r == 0:
        e_sd = ev([Y.dma_start(T.SD[:, 0:64, :], T.letter[:]), S.dma_start(T.SD[:, 64:128, :], T.runs[:])], 16)
    e_x2 = ev([Y.dma_start(T.X2[:, 0:32], T.kids[0::2, 1024:2048]), S.dma_start(T.X2[:, 32:64], T.kids[1::2, 1024:2048])], 16)
    e_q = ev([Y.dma_start(T.QI[:, 0:8], T.top[:]), S.dma_start(T.QI[:, 8:16], T.off[:])], 16)
    wait("Y", e_winv, e_wing)
    wait("S", e_winv, e_wing)
    e_win = ev([Y.dma_start(T.WIN[0::16, :], T.kids[:, 0:1024]), S.dma_start(T.WIN[1::16, :], T.kids[:, 1:1025])], 16)
    e_sy = arr("S", 0)
    if r == 0:
        e_sy = ev([Y.dma_start(T.SY[0:64, :], T.letter[0:2, :]), Y.dma_start(T.SY[64:128, :], T.runs[0:2, :])], 16)

    e_px = ev([g.iota(T.PX[:, 0:1], [[0, 1]], 0, 1)])
    if r == 0:
        nsel = 17
        e_ts = ev([fiota(T.TS[:, 0:8], [[32, 4], [1, 2]], 0, -1), fiota(T.TS[:, 8:9], [[0, 1]], 1, 0),
                   fiota(T.TS[:, 9:17], [[32, 4], [1, 2]], 16, -1)])
    else:
        nsel = 16
        e_ts = ev([fiota(T.TS[:, 0:16], [[16, 2], [1, 2], [32, 4]], 0, -1)])
    e_j1 = ev([fiota(T.J1[:], [[0, 8], [1, 4]], 1, 0)])
    e_one = ev([V.memset(T.ONE[:], 1.0)])
    e_pad = ev([V.memset(T.GS[:, 0:96], 0.0), V.memset(T.GS[:, 1120:1216], 0.0)])
    wait("V", e_px)
    p = T.PX[:, 0:1]
    e_fi = ev([ts(T.FI[:, 0:1], p, 15, None, AND), ts(T.FI[:, 1:2], p, 5, None, SHR), ts(T.FI[:, 2:3], p, 4, 1, SHR, AND),
               ts(T.FI[:, 3:4], p, 3, None, AND), ts(T.FI[:, 4:5], p, 3, 1, SHR, AND), ts(T.FI[:, 5:6], p, 7, None, AND),
               ts(T.FI[:, 6:7], p, 31, None, AND), ts(T.FI[:, 7:8], p, 11, None, AND),
               ts(T.FI[:, 8:9], p, 5, 1, SHR, AND)])
    wait("V", e_ts)
    e_sel = ev([ts(T.SEL[:, 0:nsel], T.TS[:, 0:nsel], 0.0, None, EQ)])
    wait("V", e_fi, e_one)
    e_fe = ev([V.tensor_copy(T.FE[:, 0:9], T.FI[:, 0:9])])
    e_iob = ev([V.tensor_tensor_scan(T.IOB[:], T.ONE[:], T.ONE[:], -257.0, MUL, ADD)])
    f_t, f_blk, f_c, f_r4, f_b3, f_m8, f_x32, f_p11, f_cp = [T.FE[:, i:i + 1] for i in range(9)]
    wait("S", e_one)
    e_zero = ev([act(b[:], T.ONE[:, 0:128], 0.0) for b in (T.SELW, T.PI, T.PC)])

    def pack_queries():
        wait("V", e_q)
        return ev([V.tensor_copy(T.KQ[:, 32 + 16 * r:40 + 16 * r], T.QI[:, 0:8]),
                   ts(T.KQ[:, 40 + 16 * r:48 + 16 * r], T.QI[:, 8:16], 1.0, None, ADD)])

    own_q = T.KQ[:, 32 + 16 * r:48 + 16 * r]
    if r == 0:
        wait("g", e_sd)
        send("S", lambda d: T.SD[d])
    else:
        e_ql = pack_queries()
        wait("g", e_ql)
        send("Q", lambda d: own_q)
    e_i16 = ev([fiota(T.I16[:], [[8, 2], [0, 2], [2, 4]], 0, 0), fiota(T.C64[:], [[0, 8], [1, 2], [0, 4]], 0, 0),
                fiota(T.R64[:], [[1, 8], [0, 8]], 0, 0)])

    def small_constants():
        wait("V", e_fe, e_j1)
        return ev([ts(T.FD[:, 13:14], f_x32, -16.0, 248.5, MUL, ADD),
                   ts(T.MK[:], T.J1[:, 0:4], -1.0, f_blk, ADD, EQ),
                   ts(T.FD[:, 0:1], f_p11, 3.0, None, EQ),
                   ts(T.FD[:, 1:2], f_t, 15.0, 512.0, EQ, MUL),
                   ts(T.FD[:, 2:3], f_t, 11.0, 8192.0, EQ, MUL),
                   ts(T.FD[:, 3:4], f_c, 2.0, None, MUL),
                   ts(T.FD[:, 4:5], f_c, 2.0, 1.0, MUL, ADD),
                   ts(T.FD[:, 5:6], f_blk, 2.0, None, OP.is_ge),
                   ts(T.FD[:, 6:7], f_r4, 16.0, f_b3, MUL, ADD),
                   ts(T.FD[:, 7:8], f_c, 2.0, f_b3, MUL, ADD),
                   ts(T.FD[:, 8:9], f_c, 2.0, f_cp, MUL, ADD),
                   ts(T.FD[:, 9:10], f_blk, 2.0, None, OP.is_lt),
                   ts(T.FD[:, 10:11], f_t, 0.0, None, EQ),
                   ts(T.FD[:, 11:12], f_t, 1.0, 256.0, EQ, MUL),
                   ts(T.FD[:, 12:13], f_t, 2.0, 65536.0, EQ, MUL),
                   ts(T.EL[:], T.ONE[:, 0:32], f_t, None, MUL)])

    wait("V", e_x2)
    e_xt = ev([V.transpose(T.XT[:, 32 * c:32 * c + 32], T.X2[:, c::2]) for c in range(2)])
    if r == 0:
        e_ql = pack_queries()
    wait("V", e_xt)
    if r == 0:
        e_u1 = ev([ts(T.U1[:, 2 * h + c::4], T.XT[:, 32 * c + 16 * h:32 * c + 16 * h + 16], 2.0, None, MUL)
                   for h in range(2) for c in range(2)])
        wait("V", e_ql)
        e_q3 = ev([V.tensor_copy(T.U3[:, d, 32:48], own_q) for d in range(1, 4)])
    else:
        e_u1 = ev([ts(T.U1[:, c::2], T.XT[:, 32 * c:32 * c + 32], 2.0, None, MUL) for c in range(2)])
    wait("V", e_u1, e_win)
    wait("S", e_u1, e_win)
    e_gv = ev([ts(T.GS[:, 96:608], T.WIN[:, 0:1024].indirect(T.U1[:, 0:32]), -256.0, None, ADD)])
    e_gs = ev([act(T.GS[:, 608:1120], T.WIN[:, 0:1024].indirect(T.U1[:, 32:64]), bias=-256.0)])
    wait("P", e_sel, e_pad, e_gv)
    mm = []
    if r == 0:
        for k in range(-1, 16):
            if k == 7:
                wait("P", e_gs)
            lhs = T.GS[:, 96 + 64 * k:224 + 64 * k]
            if k == -1:
                mm.append(P.matmul(T.psS[:, 143:271:16], lhs, T.SEL[:, 9:17], True, True))
            elif k == 15:
                mm.append(P.matmul(T.psS[:, 15:128:16], lhs, T.SEL[:, 0:8], True, True))
            else:
                mm.append(P.matmul(T.psS[:, k:k + 272:16], lhs, T.SEL[:, 0:17], True, True))
    else:
        for k in range(-3, 32):
            if k == 0:
                e_head = ev(mm)
                mm = []
            if k == 13:
                wait("P", e_gs, e_head)
            n0, n1, m = 4 * max(0, -k), 4 * min(4, 32 - k), 32 * min(4, 32 - k)
            mm.append(P.matmul(T.psS[0:m, 32 * n0 + k + 3:32 * (n1 - 1) + k + 4:32], T.GS[:, 96 + 32 * k:96 + 32 * k + m],
                               T.SEL[:, n0:n1], True, True))
    e_mm = ev(mm)
    if r == 0:
        wait("V", e_mm)
        e_u2 = ev([ts(T.U3[0:64, :, 0:32], T.psS[0:64, 0:128], 256.0, None, ADD),
                   ts(T.U3[64:128, :, 0:32], T.psS[64:128, 143:271], 256.0, None, ADD)])
        e_c1 = small_constants()
        wait("g", e_q3, e_u2)
        send("K", lambda d: T.U3[:, d, :])
    else:
        e_c1 = small_constants()
        wait("V", e_mm)
        e_u2 = ev([ts(T.U2[32 * b:32 * b + 32, :], T.psS[32 * b:32 * b + 32, 127 * b + 3:127 * b + 131], 256.0, None, ADD)
                   for b in range(4)])
        wait("g", e_u2)
        send("K", lambda d: T.U2[:, 32 * d:32 * d + 32])
    e_lw0 = ev([g.iota(T.LW[:], [[0, 512]], 0, 0)])
    e_cc1 = ev([fiota(T.CC[:], [[0, 128]], 1, 0)])

    def lists(l, a, b):
        if l != r:
            return T.KQ[:, kcol(l) + a:kcol(l) + b]
        return T.U3[:, 0, a:b] if r == 0 else T.U2[:, 32 * r + a:32 * r + b]

    d_a37, d_512, d_iw, d_k0, d_k1, d_hi, d_ql, d_code, d_k4, d_lo, d_l0, d_l1, d_l2, d_mid = [T.FD[:, i:i + 1] for i in range(14)]
    wait("S", e_c1, e_iob, e_zero)
    e_xd = ev([act(T.XD[:], T.IOB[:], bias=d_mid, func=AF.Abs)])
    e_jm = ev([act(T.JM[:, 32 * H + 16 * y:32 * H + 16 * y + 16], T.J1[:, 16 * y:16 * y + 16],
                   T.MK[:, 2 * y + H:2 * y + H + 1], -1.0) for H in range(2) for y in range(2)])
    e_c2 = ev([act(T.SELW[:, 3:64:16], T.ONE[:, 0:4], T.MK[:, 2:3]), act(T.SELW[:, 67:128:16], T.ONE[:, 0:4], T.MK[:, 3:4]),
               act(T.PI[:, 11::16], T.ONE[:, 0:8]), act(T.PC[:, 3::16], T.ONE[:, 0:8], -256.0),
               act(T.PC[:, 7::16], T.ONE[:, 0:8], -256.0), act(T.PC[:, 15::16], T.ONE[:, 0:8])])
    e_jm4 = ev([act(T.JM[:, 64 + 16 * y:80 + 16 * y], T.J1[:, 16 * y:16 * y + 16], (d_lo, d_hi)[y], -1.0) for y in range(2)])
    wait("V", e_c1)
    e_sw = ev([ts(T.SW[:, 0:1], d_a37, d_512, None, ADD), ts(T.SW[:, 1:2], d_code, -2.0, None, ADD),
               ts(T.SW[:, 2:3], d_l0, d_l1, d_l2, ADD, ADD)])
    sw, lw = T.SW[:, 0:1], T.SW[:, 2:3]
    wait("V", e_xd)
    e_xm = ev([ts(T.XM[:], T.XD[:], 8.0, d_hi, OP.is_lt, MUL)])
    wait("V", e_sw, e_jm)
    jm = T.JM[:, 0:64]
    e_zv = ev([ts(T.ZM[:, 256 * c + 2:256 * c + 256:4], jm, (d_k0, d_k1)[c], lw, EQ, MUL) for c in range(2)])
    z = []
    for c in range(2):
        z += [ts(T.ZM[:, 256 * c + 1:256 * c + 256:4], jm, (d_k0, d_k1)[c], sw, OP.is_gt, MUL),
              ts(T.ZM[:, 256 * c + 3:256 * c + 256:4], jm, f_c, d_a37, EQ, MUL)]
    wait("V", e_zv)
    e_zm = ev(z + [ts(T.ZM[:, 0::4], T.ZM[:, 2::4], -1.0, None, MUL)])

    def zm(H, c):
        return T.ZM[:, 256 * c + 128 * H:256 * c + 128 * H + 128]

    banks = [(T.pb0, T.pb1), (T.pb2, T.pb3), (T.pb4, T.pb5), (T.pb0, T.pb1), (T.pb2, T.pb3)]

    def open_window(w):
        for H in range(2):
            P.matmul(banks[w][H][:, 0:256], T.PI[0:1, :], T.IOB[0:1, 256 * H:256 * H + 256], True, False)
            if w == 3:
                P.matmul(banks[w][H][:, 0:256], T.PC[0:1, :], T.ONE[0:1, 0:256], False, False)

    def close_window(w, e0, e1):
        W = T["W%d" % w]
        if w == 0:
            wait("S", e0)
            ev0 = ev([act(W[:, 0:256], banks[w][0][:, 0:256])])
        else:
            wait("V", e0)
            ev0 = ev([V.tensor_copy(W[:, 0:256], banks[w][0][:, 0:256])])
        wait("S", e1)
        ev1 = ev([act(W[:, 256:512], banks[w][1][:, 0:256])])
        return ev0, ev1

    wait("P", e_c2, e_iob, e_one)
    for w in range(3):
        open_window(w)
    wait("V", e_sy, e_xm)
    ex = [ev([V.tensor_tensor(T.EX[:, 256 * H:256 * H + 256], T.SY[:, 0:16].indirect(T.EL[:, 16 * H:16 * H + 16]),
                              T.XM[:, 256 * H:256 * H + 256], MUL)]) for H in range(2)]
    em = []
    for H in range(2):
        wait("P", ex[H])
        em.append(ev([P.matmul(banks[0][H][:, 0:256], T.SELW[:], T.EX[:, 256 * H:256 * H + 256], False, True)]))
    ew = close_window(0, em[0], em[1])
    e_pl = ev([ts(T.PL[0:64, 0:16], T.SY[0:64, :], 255, None, AND), ts(T.PL[0:64, 16:32], T.SY[0:64, :], 8, 255, SHR, AND),
               ts(T.PL[0:64, 32:48], T.SY[0:64, :], 16, None, SHR)])
    wait("Y", e_pl, e_lw0)
    e_lw = ev([Y.dma_start(T.LW[16 * q + j::64, :], T.PL[0:64, 16 * j:16 * j + 16]) for q in range(4) for j in range(3)], 16)
    wait("V", e_i16, e_jm4)
    jm4 = T.JM[:, 64:96]
    e_a1 = ev([ts(T.PE4[:, 0:32], jm4, d_k4, sw, OP.is_gt, MUL), ts(T.PE4[:, 32:64], jm4, d_k4, d_iw, EQ, MUL)])
    a1 = [ts(T.A4[:, 1::4], jm4, d_k4, sw, OP.is_gt, MUL), ts(T.A4[:, 3::4], jm4, f_c, d_a37, EQ, MUL)]
    e_qc = ev([ts(T.QLS[:], T.I16[:], d_ql, None, ADD),
               ts(T.QM[:, 0:64], T.C64[:], d_code, T.MK[:, r:r + 1], EQ, MUL),
               ts(T.QM[:, 64:128], T.C64[:], T.SW[:, 1:2], T.MK[:, r:r + 1], EQ, MUL)])
    wait("V", e_a1)
    a1 += [V.tensor_tensor(T.A4[:, 2::4], T.PE4[:, 32:64], T.PE4[:, 0:32], OP.subtract),
           V.tensor_tensor(T.A4[:, 0::4], T.PE4[:, 0:32], T.PE4[:, 32:64], OP.subtract)]
    e_am = ev(a1)

    wait("P", e_zm)
    for l in range(4):
        W, G = T["W%d" % l], T["G%d" % l]
        ek = e_u2 if l == r else arr("K", l)
        wait("V", ek, *ew)
        wait("S", ek, *ew)
        e0 = ev([V.tensor_copy(G[:, 0:256], W[:, 0:512].indirect(lists(l, 0, 16)))])
        e1 = ev([act(G[:, 256:512], W[:, 0:512].indirect(lists(l, 16, 32)))])
        if l == 0:
            wait("V", e_ql, e_qc, *[arr("Q", s) for s in range(1, 4)])
            e_qf = ev([V.tensor_copy(T.QF[:], T.KQ[:, 32:96])])
            e_rh = ev([ts(T.RH4[:], T.R64[:], f_m8, None, EQ), ts(T.M4[:], T.C64[:], f_c, None, EQ)])
            wait("V", e_qf)
            e_qt = ev([V.tensor_tensor(T.QG[:, 0:128], T.QF[:, 0:64].indirect(T.QLS[:, 0:8]), T.QM[:], MUL)])
        if l == 1:
            e_qo = ev([V.tensor_tensor(T.QG[:, 128:256], T.QF[:, 0:64].indirect(T.QLS[:, 8:16]), T.QM[:], MUL)])
        if l == 2:
            wait("V", e_qm, e_rh)
            e_nu = ev([V.tensor_copy(T.NU0[:], T.psQ[:, 0:16])])
            e_o = ev([V.tensor_tensor(T.O0[:], T.psQ[:, 64:128], T.M4[:], MUL)])
        em = []
        for H in range(2):
            out = banks[l + 1][H][:, 0:256]
            if l == 0:
                wait("P", e0, e1)
                P.matmul(out, zm(H, 0), G[:, 0:256], False, False)
                em.append(ev([P.matmul(out, zm(H, 1), G[:, 256:512], False, True)]))
            else:
                wait("P", e_am, (e0, e1)[H])
                em.append(ev([P.matmul(out, T.A4[:], G[:, 256 * H:256 * H + 256], l == 3, True)]))
        if l == 1:
            open_window(3)
            wait("P", e_qt, e_qo, e_rh)
            e_qm = ev([P.matmul(T.psQ[:, 0:16], T.QG[:, 0:128], T.RH4[:, 0::4], True, True),
                       P.matmul(T.psQ[:, 64:128], T.QG[:, 128:256], T.RH4[:], True, True)])
        ew = close_window(l + 1, em[0], em[1])

    for H in range(2):
        for c in range(2):
            P.matmul(banks[2][H][:, 0:256], zm(H, c), T.G0[:, 256 * c:256 * c + 256], c == 0, False)

    wait("S", *ew)
    wait("V", e_cc1)
    for d in range(4):
        W, NU, GD, TT = (T.W4, T.W3, T.W2, T.T0)[d], T["NU%d" % d], T["GD%d" % d], T["TT%d" % d]
        O, R, TU = T["O%d" % d], T["R%d" % d], T["TU%d" % d]
        wait("S", e_nu)
        e_gd = ev([act(GD[:], W[:, 0:512].indirect(NU[:, 0:16]))])
        if d == 0:
            wait("S", e_lw)
            e_lg = [ev([act(T.LG[:, 256 * c:256 * c + 256], T.LW[:, 0:512].indirect(lists(0, 16 * c, 16 * c + 16)))])
                    for c in range(2)]
            em = []
            for c in range(2):
                wait("P", e_lg[c])
                for H in range(2):
                    i = P.matmul(banks[2][H][:, 0:256], zm(H, c), T.LG[:, 256 * c:256 * c + 256], False, c == 1)
                    if c == 1:
                        em.append(i)
            e_t0m = ev(em)
        if d == 2:
            wait("S", e_t0m)
            e_t0 = ev([act(T.T0[:, 256 * H:256 * H + 256], banks[2][H][:, 0:256]) for H in range(2)])
            wait("S", e_t0)
        wait("V", e_gd)
        e_tt = ev([V.transpose(TT[:], GD[:])])
        wait("V", e_tt, e_o)
        e_cc = ev([V.tensor_tensor(T.CC[:, 1::2], TT[:, 1::4], O[:], OP.is_ge)])
        wait("V", e_cc)
        e_r = ev([V.tensor_tensor_scan(R[:], T.CC[:], TT[:, 0::2], 0.0, MUL, ADD)])
        wait("V", e_r)
        if d < 3:
            N2 = T["NU%d" % (d + 1)]
            e_nu = ev([ts(N2[:], R[:, 7::8], 1.0 / 8192.0, 256.4, MUL, ADD)])
            e_t = ev([V.tensor_tensor(TU[:, 0:16], R[:, 7::8], O[:, 0::4], ADD)])
            wait("V", e_nu)
            e_u = ev([ts(TU[:, 16:32], N2[:], -256.0, -8192.0, ADD, MUL)])
            wait("V", e_t, e_u)
            O2 = T["O%d" % (d + 1)]
            e_o = ev([V.tensor_tensor(O2[:, k::4], TU[:, 0:16], TU[:, 16:32], ADD) for k in range(4)])
        else:
            e_ans = ev([V.tensor_copy(T.ANS[:], R[:, 15::16])])

    wait("g", e_ans)
    send("A", lambda d: T.ANS[:])
    wait("S", e_ans)
    st = [S.dma_start(T.y[2 * r:2 * r + 2, :], T.ANS[r::4, :])]
    order = direct + [d for d, _ in far]
    for i, d in enumerate(order):
        q = "YYS"[i]
        wait(q, arr("A", d))
        st.append(Q[q].dma_start(T.y[2 * d:2 * d + 2, :], T.AD[d, r::4, :]))
    e_st = ev(st, 16)
    wait("Y", e_st)
    g.wait_ge(T.sem.sent, sent[0])
